import numpy as np, ml_dtypes
CORES = [113,118,241,246]
N = 4
BF = ml_dtypes.bfloat16
def gentries(a):
    return np.ascontiguousarray(a.reshape(8, 16, -1).transpose(0, 2, 1)).reshape(8, -1)
def gtable(e):
    e = np.asarray(e); return np.ascontiguousarray(e.reshape(8, -1, 16).transpose(0, 2, 1)).reshape(128, -1).astype(np.int32)
V0, M, RO, H, S = 1024, 128, 3, 3, 2
V = V0 + RO * M
def parts(rng):
    m = rng.integers(0, 256, (N, 8, 12, 16)); c = rng.integers(0, 12, (N, 8, V, 1))
    x = np.clip(np.take_along_axis(m, c, 2) + rng.integers(-60, 61, (N, 8, V, 16)), 0, 255)
    y = rng.integers(0, 257, (N, 8, V0, 16)) * 0.00390625
    nx = np.argsort(rng.random((N, 8, 8, V0)), axis=-1)
    few = np.take_along_axis(rng.integers(0, V0, (N, 8, 6)), rng.integers(0, 6, (N, 8, RO * M)), 2).reshape(N, 8, RO, M)
    st = np.where(rng.random((N, 8, RO, M)) < 0.25, few, rng.integers(0, V0, (N, 8, RO, M)))
    return x, y, nx, st
def pack(x, y, nx, st):
    return {"x": np.ascontiguousarray(x.transpose(0, 1, 3, 2)).reshape(N, 128, V).astype(np.float32).astype(BF),
            "y0": np.ascontiguousarray(y.transpose(0, 1, 3, 2)).reshape(N, 128, V0).astype(np.float32).astype(BF),
            "nx0": np.ascontiguousarray(nx.reshape(N, 64, V0)).astype(np.int32), "st": np.stack([gtable(a.reshape(8, -1)) for a in st])}
def setup_inputs(rng):
    return pack(*parts(rng))
def setup_inputs_spread(rng):
    x, y, nx, st = parts(rng)
    x = (np.exp2(rng.integers(0, 9, (N, 8, V, 1))) * rng.random((N, 8, V, 16))).astype(np.int64)
    y = rng.integers(128, 256, (N, 8, V0, 16)) * np.exp2(-7.0 - rng.integers(1, 4, (N, 8, V0, 1)))
    y = y * (rng.random((N, 8, V0, 1)) > 0.0625)
    u = 4 * rng.integers(32, 64, (N, 2, V0, 16)) + 1; u[:, :, 1::2] += 2
    y[:, 1::4] = u * 0.0001220703125
    nx[:, 1::4, :, 0::2] = 2 * np.argsort(rng.random((N, 2, 8, V0 // 2)), axis=-1) + 1
    nx[:, 1::4, :, 1::2] = 2 * np.argsort(rng.random((N, 2, 8, V0 // 2)), axis=-1)
    st = (V0 * rng.random((N, 8, RO, M)) ** 3).astype(np.int64)
    return pack(x, y, nx, st)
def link(p, a, b):
    i = np.flatnonzero(p == b)[0]; p[i] = p[a]; p[a] = b
def setup_inputs_ends(rng):
    x, y, nx, st = parts(rng); L = V0 - 1
    for q in range(N):
        for g in range(8):
            for k in range(8):
                if k % 4 in (0, 2): link(nx[q, g, k], 0, L)
                if k % 4 in (1, 2): link(nx[q, g, k], L, 0)
                if k % 4 == 3: link(nx[q, g, k], L, L); link(nx[q, g, k], 0, 0)
    pv = np.argsort(nx, axis=-1)
    e = 255 * rng.integers(0, 2, (N, 8, V, 16)); e[:, 1::2] = 255 * rng.integers(0, 2, (N, 4, V, 1))
    n = (rng.random((N, 4, V, 16)) < 0.25) * rng.integers(1, 3, (N, 4, V, 16)); e[:, 0::2] += np.where(e[:, 0::2] > 0, -n, n)
    for q in range(N):
        for g, b in ((3, 0), (5, 255), (7, 0)):
            e[q, g, nx[q, g, :, L]] = b; e[q, g, pv[q, g, :, L]] = b
    e[:, :, 0] = 0; e[:, :, L] = 0
    for v in (V0, V0 + M - 1, V - M, V - 1): e[:, :, v] = 255
    st = np.where(rng.random(st.shape) < 0.8, L * rng.integers(0, 2, st.shape), st); st[..., 0] = 0; st[..., M - 1] = L
    p = np.full((1, 8, 1, 1), 0.5); p[0, 2] = 0.96875; p[0, 7] = 0.96875; p[0, 3] = 0.03125
    y = (rng.random((N, 8, V0, 16)) < p) * 1.0
    return pack(e, y, nx, st)
def corner(rng, c):
    a = np.arange(V0); o = rng.permutation(V0); p = np.arange(V0)
    if c == 0: return a
    if c == 1: return (a + 1) % V0
    if c == 2: return (a - 1) % V0
    if c == 3: return a ^ 1
    if c == 4: return V0 - 1 - a
    if c == 5: p[o] = np.roll(o, -1)
    if c == 6: p[o[0::2]] = o[1::2]; p[o[1::2]] = o[0::2]
    if c == 7: h = o[:V0 // 2]; p[h] = np.roll(h, 1)
    return p
def setup_inputs_corners(rng):
    x, y, nx, st = parts(rng)
    for q in range(N):
        for g in range(8):
            o = rng.permutation(8)
            for k in range(8): nx[q, g, k] = corner(rng, o[k])
        nx[q, q % 8] = np.arange(V0); nx[q, (q + 1) % 8] = corner(rng, 5)
    st = np.where(rng.random(st.shape) < 0.4, rng.choice(np.array([0, 1, V0 - 2, V0 - 1]), st.shape), st)
    same = np.take_along_axis(x, st.reshape(N, 8, RO * M, 1), 2)
    x[:, :, V0:] = np.where(rng.random((N, 8, RO * M, 1)) < 0.3, same, x[:, :, V0:])
    y[:, 4] = 1.0; y[:, 5] = 0.0
    return pack(x, y, nx, st)
def setup_inputs_crowd(rng):
    x, y, nx, st = parts(rng)
    for q in range(N):
        for g in range(8):
            kind = (g + q) % 5; base = rng.integers(0, 256, 16); s = rng.integers(0, V0, 4)
            for t in range(RO):
                odd = (-1, int(rng.integers(0, M)), 0, M - 1, -1)[kind]; alike = np.arange(M) != odd; a = V0 + t * M
                x[q, g, a:a + M][alike] = np.clip(base + rng.integers(-2, 3, 16), 0, 255)
                st[q, g, t][alike] = s[0]
                if kind == 4: st[q, g, t] = s[rng.integers(0, 4, M)]
    return pack(x, y, nx, st)
def setup_inputs_ties(rng):
    x, y, nx, st = parts(rng)
    x = 100 + rng.integers(0, 2, (N, 8, V, 16))
    x[:, 1::2] = np.take_along_axis(rng.integers(0, 256, (N, 4, 3, 16)), rng.integers(0, 3, (N, 4, V, 1)), 2)
    one = 255 - (np.arange(16) == rng.integers(0, 16, (N, V, 1))).astype(np.int64)
    x[:, 2] = np.where(rng.random((N, V, 1)) < 0.3, one, 255); x[:, 2, V0:] = 0
    x[:, 6] = rng.integers(0, 2, (N, V, 16)); x[:, 6, V0:] = 255
    c = rng.integers(0, 3, (N, V, 1))
    x[:, 4] = np.where(c == 0, 0, np.where(c == 1, 255, one)); x[:, 4, V0:] = rng.integers(1, 20, (N, RO * M, 16))
    return pack(x, y, nx, st)
def check_ranges(d):
    bad = []
    w = dict((k, np.asarray(d[k]).astype(np.float64)) for k in ("x", "y0", "nx0", "st"))
    for k, lo, hi in (("x", 0, 255), ("y0", 0, 1), ("nx0", 0, V0 - 1), ("st", 0, V0 - 1)):
        if not (np.min(w[k]) >= lo and np.max(w[k]) <= hi): bad.append("range of " + k)
    if np.any(w["x"] != np.floor(w["x"])): bad.append("x is not whole")
    if np.any((w["y0"] > 0) & (w["y0"] < 2.0 ** -8)): bad.append("y0 is too small and not 0")
    if np.any(np.sort(w["nx0"], axis=-1) != np.arange(V0)): bad.append("a row of nx0 is not a permutation")
    return bad
def dist(a, b):
    return np.add.reduce(np.abs(a - b), axis=-1)
def search(x, nx, pv, xv, p):
    m = np.arange(M)
    for h in range(H):
        w = np.concatenate([nx[:, p], pv[:, p]])
        e = dist(x[w], xv); i = np.argmin(e, axis=0)
        p = np.where(e[i, m] < dist(x[p], xv), w[i, m], p)
    return p
def enter(x, nx, pv, v, b):
    n2 = nx.copy(); p2 = pv.copy()
    for k in range(8):
        c = nx[(k + 1) % 8, b]; f = nx[k, c]; a = pv[k, c]
        ahead = dist(x[c], x[f]) - dist(x[v], x[f]); back = dist(x[c], x[a]) - dist(x[v], x[a])
        tail, first = np.unique(np.where(ahead >= back, c, a), return_index=True)
        w = v[first]; head = nx[k, tail]
        n2[k, v] = v; p2[k, v] = v
        n2[k, tail] = w; n2[k, w] = head; p2[k, head] = w; p2[k, w] = tail
    return n2, p2
def reference(x, y0, nx0, st):
    xs = np.ascontiguousarray(x.astype(np.float32).astype(np.int64).reshape(N, 8, 16, V).transpose(0, 1, 3, 2))
    ys = np.zeros((N, 8, V, 16)); ys[:, :, :V0] = y0.astype(np.float64).reshape(N, 8, 16, V0).transpose(0, 1, 3, 2)
    nx = np.tile(np.arange(V), (N, 8, 8, 1)); nx[..., :V0] = nx0.reshape(N, 8, 8, V0); pv = np.argsort(nx, axis=-1)
    sl = np.stack([gentries(a) for a in st]).astype(np.int64).reshape(N, 8, RO, M)
    for t in range(RO):
        v = V0 + t * M + np.arange(M); have = V0 + (t + 1) * M
        b = np.zeros((N, 8, M), np.int64); got = np.zeros((N, 8, M, 16))
        for r in range(N):
            q = (r + 1 + t) % N
            for g in range(8):
                b[r, g] = search(xs[r, g], nx[r, g], pv[r, g], xs[r, g, v], sl[r, g, t])
                got[r, g] = ys[q, g][search(xs[q, g], nx[q, g], pv[q, g], xs[r, g, v], sl[r, g, t])]
        for r in range(N):
            for g in range(8):
                nx[r, g], pv[r, g] = enter(xs[r, g], nx[r, g], pv[r, g], v, b[r, g])
                y = ys[r, g, :have].copy(); y[v] = got[r, g]
                for s in range(S):
                    y = 0.5 * (1.0 + y) - 0.0625 * np.add.reduce(y[nx[r, g, :, :have]] * y[pv[r, g, :, :have]], axis=0)
                ys[r, g, :have] = y
    return {"y": np.ascontiguousarray(ys.transpose(0, 1, 3, 2)).reshape(N, 128, V).astype(np.float32), "nx": nx.reshape(N, 64, V).astype(np.float32)}

def check_inputs(d):
    bad = list(check_ranges(d))
    if not bad:
        for name, y in reference(**d).items():
            for q in range(N):
                v = np.abs(np.asarray(y[q], np.float64)); s = np.sqrt(np.mean(v * v))
                if v.max() > 3 * s or s < 2.0 ** -2: bad.append('%s of rank %d is uneven or too small' % (name, q))
    return bad

@@ -1,0 +1,567 @@
+from concourse.bass import DstId, RemoteDMATransfer
+from concourse.mybir import AluOpType as ALU, ActivationFunctionType as ACT
+
+N, V0, M, RO, HOPS, SWEEPS = 4, 1024, 128, 3, 3, 2
+V = V0 + RO * M
+F32, BF, I32, U16, F16 = "float32", "bfloat16", "int32", "uint16", "float16"
+ZW = 144
+CU = 64
+NBUF = 3
+ENC, OFF = 4096, 16384
+BIG = 33554432.0
+
+
+def sb(w, d):
+    return ("sbuf", [128] + (list(w) if isinstance(w, (list, tuple)) else [w]), d)
+
+
+SCRATCH = {
+    "W": sb(16 * V, F32), "PS": sb(2 * NBUF * 16 * CU, F32), "mv": sb(2048, BF), "NWB": sb(128, F32), "yA": sb(V, F32), "yB": sb(V, F32),
+    "NBraw": sb(V, F32), "NBi": sb(V, I32), "NBf": sb(V, F32), "NB16": sb(V, U16),
+    "AL0": sb(V // 2, U16), "AL1": sb(V // 2, U16), "BL0": sb(V // 2, U16), "BL1": sb(V // 2, U16),
+    "VID": sb(V, F32), "xc": sb(V, BF), "xr": sb(RO * M, BF),
+    "sti": sb(24, I32), "st16": sb(24, U16), "str16": sb(24, U16),
+    "Lraw": sb(512, I32), "L16": sb(512, U16), "IV": sb(V0, F32), "WENC": sb(V0, F32),
+    "a0": sb(2048, BF), "a1": sb(2048, BF), "m0": sb(2048, BF), "m1": sb(2048, BF),
+    "ones": sb(2048, BF), "EXP": sb(2048, BF), "SELU": sb(1024, BF), "SEL": sb(1024, F16),
+    "Z": sb(16 * ZW, F16), "Zf": sb(ZW, F32), "RM": sb(16, F32),
+    "Ib": sb(128, BF), "If": sb(128, F32), "Ih": sb(128, F32), "In": sb(128, F32),
+    "HR": sb(256, BF), "PR": sb(384, BF), "NEG": sb(8, BF), "BOX": sb(256, BF), "BO2": sb(16, BF), "BOP": sb(8, BF),
+    "C2": sb(64, BF), "RST": sb(256, F32), "SC": sb(16, F32), "TRI": sb(128, BF), "U": sb(64, BF),
+    "ci": sb(16, I32), "cf": sb(24, F32), "WL": sb(64, F32), "WLe": sb(64, F32), "BASE": sb(128, F32),
+    "G1": sb(1024, F16), "E": sb(1024, BF), "cb": sb(128, F16), "brep": sb(128, F16), "nbrep": sb(128, F16),
+    "CL16": sb(64, U16), "FA16": sb(128, U16), "CH": sb(128, BF), "LX": sb([16, 2, 8], BF),
+    "P1": sb(256, F32), "P2": sb(256, F32), "t1": sb(256, F32), "t2": sb(256, F32), "s1": sb(128, F32), "s2": sb(128, F32),
+    "HT": sb(128, F32), "O16": sb(128, U16), "win": sb(64, F32), "nw": sb(128, F32), "NEW": sb(128, F16),
+    "ysend": sb(RO * M, F32),
+}
+for _s in "01":
+    SCRATCH.update({"pl" + _s: sb(8, U16), "c16" + _s: sb(128, U16), "cF" + _s: sb(128, F32), "hr" + _s: sb(128, BF),
+                    "xT" + _s: sb(128, BF), "sc" + _s: sb(256, F32), "best" + _s: sb(16, I32),
+                    "low" + _s: sb(16, I32), "lowb" + _s: sb(16, BF), "sd" + _s: sb(64, F32),
+                    "ia" + _s: sb(128, BF), "im" + _s: sb(128, BF), "iF" + _s: sb(128, F32), "ih" + _s: sb(128, BF)})
+BANKS = ["SW0", "SW1", "VR00", "VR01", "VR10", "VR11", "K0", "K1"]
+for _b in BANKS:
+    SCRATCH[_b] = ("psum", [128, 512], F32)
+NDMA = 40
+SEMAPHORES = ["eV", "eS", "eP", "eG", "sent", "rx", "rst", "ry0", "ry1", "ry2"] + ["d%d" % i for i in range(NDMA)]
+
+CYC, GA, SCA, PEC, SYNC = 1.0e-3, 1.6, 3.8, 0.5e-3, 0.12
+
+
+def plan_order(ops):
+    n = len(ops)
+    succ = [[] for _ in range(n)]
+    for i, o in enumerate(ops):
+        for d in o["deps"]:
+            succ[d].append(i)
+    prio = [0.0] * n
+    for i in range(n - 1, -1, -1):
+        prio[i] = ops[i]["cost"] + ops[i]["lat"] + max([prio[j] + SYNC for j in succ[i]] + [0.0])
+    left = [len(o["deps"]) for o in ops]
+    rdy = [0.0] * n
+    ready = [i for i in range(n) if left[i] == 0]
+    free, order = {}, []
+    while ready:
+        est = dict((i, max(rdy[i], free.get(ops[i]["eng"], 0.0))) for i in ready)
+        first = min(ready, key=lambda i: (est[i], -prio[i]))
+        eng = ops[first]["eng"]
+        near = [i for i in ready if ops[i]["eng"] == eng and est[i] <= est[first] + 0.3]
+        i = max(near, key=lambda j: (prio[j], -j))
+        ready.remove(i)
+        order.append(i)
+        ops[i]["at"] = est[i]
+        if eng != "none":
+            free[eng] = est[i] + ops[i]["cost"]
+        done = est[i] + ops[i]["cost"] + ops[i]["lat"]
+        for j in succ[i]:
+            rdy[j] = max(rdy[j], done + SYNC)
+            left[j] -= 1
+            if left[j] == 0:
+                ready.append(j)
+    return order
+
+
+def mask_of(engs):
+    m = 0
+    for e in engs:
+        m |= 1 << e
+    return m
+
+
+def widest(engs):
+    n = 1
+    while 2 * n <= len(engs):
+        n *= 2
+    return engs[:n]
+
+
+def build_ops(g, core, T, topo):
+    rank = T.rank_of(core)
+    ops, wr_of, rd_of = [], {}, {}
+    ALL = 1 << 30
+
+    def tok(x):
+        return (x, 0, ALL) if isinstance(x, str) else x
+
+    def add(eng, fn, reads, writes, cost, lat=0.0, kind="c", after=(), sem=None):
+        i = len(ops)
+        reads = [tok(x) for x in reads]
+        writes = [tok(x) for x in writes] + [x for x in reads if x[0] in BANKS]
+        reads = [x for x in reads if x[0] not in BANKS]
+        deps, hard = set(after), set()
+        for (lst, seen) in ((reads, [wr_of]), (writes, [wr_of, rd_of])):
+            for (b, lo, hi) in lst:
+                for tab in seen:
+                    for (j, l2, h2) in tab.get(b, []):
+                        if l2 < hi and lo < h2:
+                            deps.add(j)
+                            if not (b in BANKS and eng == "P" and ops[j]["eng"] == "P"):
+                                hard.add(j)
+        for (b, lo, hi) in writes:
+            wr_of[b] = [w for w in wr_of.get(b, []) if not (lo <= w[1] and w[2] <= hi)] + [(i, lo, hi)]
+            rd_of[b] = [w for w in rd_of.get(b, []) if not (lo <= w[1] and w[2] <= hi)]
+        for (b, lo, hi) in reads:
+            rd_of.setdefault(b, []).append((i, lo, hi))
+        ops.append({"eng": eng, "fn": fn, "deps": deps, "hard": hard, "cost": cost, "lat": lat, "kind": kind, "sem": sem,
+                    "w": [x[0] for x in writes][:2]})
+        return i
+
+    def follow(i, *earlier):
+        ops[i]["deps"].update(earlier)
+
+    vq, sq, pq = g.vector, g.scalar, g.tensor
+
+    def vec(fn, r, w, n, per=1.0):
+        return add("V", lambda: [fn()], r, w, 0.06 + max(64, n * per) * CYC)
+
+    def act(out, in_, r, w, n, per=1.0, func=ACT.Copy, **kw):
+        return add("S", lambda: [sq.activation(out, in_, func, **kw)], r, w, 0.08 + max(64, n * per) * CYC)
+
+    def pool(fn, r, w, n):
+        return add("G", lambda: [fn()], r, w, 0.17 + 2 * n * CYC)
+
+    def iota(out, pat, base, w, n):
+        return pool(lambda: g.iota(out, pat, base, 0, allow_small_or_imprecise_dtypes=True), [], w, n)
+
+    def mm(lst, r, w, start=True, stop=True):
+        cost = sum(max(64, x[3]) * PEC * (4 if x[4] else 1) for x in lst)
+        last = len(lst) - 1
+        return add("P", lambda: [pq.matmul(x[0], x[1], x[2], start and n == 0, stop and n == last) for n, x in enumerate(lst)],
+                   r, w, cost + 0.05)
+
+    def dma(pairs, r, w, us, q="Y"):
+        eq = {"Y": g.sync, "S": sq, "G": g}[q]
+        return add(q, lambda: [eq.dma_start(o, i) for (o, i) in pairs], r, w, (0.1 if q != "G" else 1.0) * len(pairs), 2.0 + us, "dma")
+
+    def copy(out, in_, r, w, n, per=1.0):
+        return vec(lambda: vq.tensor_copy(out, in_), r, w, n, per)
+
+    def ts(out, in0, s1, op0, r, w, n, per=1.0, s2=None, op1=None):
+        if op1 is None:
+            return vec(lambda: vq.tensor_scalar(out, in0, s1, None, op0), r, w, n, per)
+        return vec(lambda: vq.tensor_scalar(out, in0, s1, s2, op0, op1), r, w, n, per)
+
+    def tt(out, in0, in1, op, r, w, n, per=2.0):
+        return vec(lambda: vq.tensor_tensor(out, in0, in1, op), r, w, n, per)
+
+    def scan(out, d0, d1, r, w, n):
+        return vec(lambda: vq.tensor_tensor_scan(out, d0, d1, 0.0, ALU.add, ALU.min), r, w, n)
+
+    def fill(out, val, w, n, per=1.0):
+        return vec(lambda: vq.memset(out, val), [], w, n, per)
+
+    def sel(out, in_, pat, cmp, fl, base, cm, r, w, n):
+        return pool(lambda: g.affine_select(out, in_, pat, cmp, fl, base, cm), r, w, n)
+
+    def shift(out, in_, bias, r, w, n, **kw):
+        return act(out, in_, r, w, n, 1.0, ACT.Identity, bias=bias, **kw)
+
+    def zmat(cls, tgt):
+        o = cls * ZW + 15 - tgt
+        return T.Z[:, o:o + 128]
+
+    S1, S2 = slice(0, 128, 18), slice(14, 113, 14)
+
+    dma([(T.Lraw[:, 64 * k:64 * k + 64], T.nx0[k::8, :]) for k in range(4, 8)], [], [("Lraw", 256, 512)], 0.3)
+    dma([(T.Lraw[:, 64 * k:64 * k + 64], T.nx0[k::8, :]) for k in range(4)], [], [("Lraw", 0, 256)], 0.3, "S")
+    dma([(T.m1[:, 0:V], T.x[:]), (T.sti[:], T.st[:])], [], ["m1", "sti"], 0.7)
+    dma([(T.NBi[0::2, 0:V0], T.nx0[:]), (T.NBi[1::2, 0:V0], T.nx0[:])], [], [("NBi", 0, V0)], 1.0)
+
+    early = [ts(T.xc[:], T.m1[:, 0:V], -127.0, ALU.add, ["m1"], ["xc"], V, 0.5),
+             copy(T.st16[:], T.sti[:], ["sti"], ["st16"], 24),
+             ts(T.yB[:, 0:V0], T.NBi[:, 0:V0], float(OFF), ALU.add, [("NBi", 0, V0)], ["yB", "yBodd"], V0)]
+
+    iota(T.IV[:], [[1, 64], [64, 16]], OFF, ["IV"], V0)
+    for h in range(2):
+        c = ("Lraw", 256 * h, 256 * h + 256)
+        copy(T.L16[:, c[1]:c[2]], T.Lraw[:, c[1]:c[2]], [c], [("L16", c[1], c[2])], 256)
+
+    def invert(k, a, b, on_scalar):
+        lo = V * (8 + k)
+        win = T.W[:, lo:lo + V0].indirect(T.L16[:, 64 * k + a:64 * k + b])
+        r, w = ["IV", ("L16", 64 * k, 64 * k + 64)], [("W", lo, lo + V0)]
+        if on_scalar:
+            return act(win, T.IV[:, 16 * a:16 * b], r, w, 16 * (b - a), SCA, ACT.Silu)
+        return copy(win, T.IV[:, 16 * a:16 * b], r, w, 16 * (b - a), SCA)
+
+    invert(4, 20, 64, False)
+    for k in (5, 6, 7):
+        follow(invert(k, 0, 64, False), *early)
+    last = [invert(k, 0, 64, True) for k in range(4)]
+    follow(invert(4, 0, 20, True), *last)
+    for k in range(8):
+        lo = V * (8 + k)
+        dma([(T.yB[2 * k + 1::16, 0:V0], T.W[S2, lo:lo + V0])], [("W", lo, lo + V0)], [("yBodd", k, k + 1)], 0.3)
+    ts(T.NBi[:, 0:V0], T.yB[:, 0:V0], -float(OFF), ALU.add, ["yB", "yBodd"], [("NBi", 0, V0)], V0)
+    copy(T.NBf[:, 0:V0], T.NBi[:, 0:V0], [("NBi", 0, V0)], ["NBf"], V0)
+
+    sent = [0]
+
+    def far(t):
+        return T.cores[(rank + 1 + t) % N]
+
+    def near(t):
+        return T.cores[(rank - 1 - t) % N]
+
+    def fused(src, off, dst, width, sem):
+        trs = []
+        for t in range(RO):
+            rid, pid = topo.addr(far(t), core)
+            engs = topo.engines(core, far(t))[2 * t:2 * t + 2]
+            trs.append(RemoteDMATransfer(dst_ids=[DstId(rid=rid, pnc=pid)], dma_engine_mask=mask_of(engs), remote_sem=sem,
+                                         src=src[:, off + width * t:off + width * t + width], dst=dst[:, width * t:width * t + width]))
+        sent[0] += 2 * RO
+        return lambda: [g.remote_dma_fused(trs, local_sem=T.sem.sent)]
+
+    sx = add("G", fused(T.xc, V0, T.xr, M, T.sem.rx), ["xc"], [], 2.0, 4.0, "remote")
+    add("none", None, [], ["xr"], 0.0, 0.0, "recv", [sx], ("rx", 2 * RO))
+    ss = add("G", fused(T.st16, 0, T.str16, 8, T.sem.rst), ["st16"], [], 1.0, 4.0, "remote")
+    add("none", None, [], ["str16"], 0.0, 0.0, "recv", [ss], ("rst", 2 * RO))
+
+    ci, cf = T.ci, T.cf
+
+    def col(b, j):
+        return b[:, j:j + 1]
+
+    pool(lambda: g.iota(col(ci, 0), [[0, 1]], 0, 1), [], [("ci", 0, 1)], 1)
+    vid0 = ("VID", 0, ZW)
+    iota(T.VID[:, 0:ZW], [[1, ZW]], 0, [vid0], ZW)
+    iota(T.VID[:, ZW:V], [[1, V - ZW]], ZW, [("VID", ZW, V)], V - ZW)
+    fill(T.ones[:], 1.0, ["ones"], 2048, 0.5)
+    p = [("ci", 0, 1)]
+    ts(col(ci, 1), col(ci, 0), 15, ALU.bitwise_and, p, [("ci", 1, 2)], 1)
+    ts(col(ci, 2), col(ci, 0), 1, ALU.bitwise_and, p, [("ci", 2, 3)], 1)
+    ts(col(ci, 3), col(ci, 0), 1, ALU.logical_shift_right, p, [("ci", 3, 4)], 1, 1.0, 7, ALU.bitwise_and)
+    ts(col(ci, 4), col(ci, 0), 7, ALU.bitwise_and, p, [("ci", 4, 5)], 1)
+    ts(col(ci, 5), col(ci, 0), 3, ALU.logical_shift_right, p, [("ci", 5, 6)], 1, 1.0, 1, ALU.bitwise_and)
+    ts(col(ci, 6), col(ci, 0), 112, ALU.bitwise_and, p, [("ci", 6, 7)], 1)
+    copy(cf[:, 0:7], ci[:, 0:7], ["ci"], [("cf", 0, 7)], 7)
+    c0 = [("cf", 0, 7)]
+    ts(col(cf, 7), col(cf, 2), 8.0, ALU.mult, c0, [("cf", 7, 8)], 1, 1.0, col(cf, 3), ALU.add)
+    for h in range(HOPS):
+        ts(col(cf, 14 + h), col(cf, 7), 64.0, ALU.mult, [("cf", 7, 8)], [("cf", 14 + h, 15 + h)], 1, 1.0, 64.0 * (16 * h + 1) - 128.0, ALU.add)
+        ts(col(cf, 17 + h), col(cf, 7), 64.0, ALU.mult, [("cf", 7, 8)], [("cf", 17 + h, 18 + h)], 1, 1.0, 64.0 * (16 * h + 1) + 4112.0, ALU.add)
+    ts(col(cf, 10), col(cf, 2), -1.0, ALU.mult, c0, [("cf", 10, 11)], 1, 1.0, 1.0, ALU.add)
+    ts(col(cf, 11), col(cf, 6), 15.0, ALU.add, c0, [("cf", 11, 12)], 1)
+    ts(col(cf, 12), col(cf, 4), float(V), ALU.mult, c0, [("cf", 12, 13)], 1)
+    ts(col(cf, 13), col(cf, 4), float(V), ALU.mult, c0, [("cf", 13, 14)], 1, 1.0, float(8 * V), ALU.add)
+    ts(T.RM[:], T.VID[:, 0:16], col(cf, 1), ALU.is_equal, [vid0, ("cf", 0, 7)], ["RM"], 16)
+    ts(T.Ib[:], T.VID[:, 0:128], col(cf, 0), ALU.is_equal, [vid0, ("cf", 0, 7)], ["Ib"], 128)
+    ts(T.If[:], T.VID[:, 0:128], col(cf, 0), ALU.is_equal, [vid0, ("cf", 0, 7)], ["If"], 128)
+    for (o, nm, val) in ((T.Ih[:], "Ih", 0.5), (T.In[:], "In", -0.0625), (T.HR[:, 0:128], ("HR", 0, 128), -1.0),
+                         (T.HR[:, 128:256], ("HR", 128, 256), 1.0 / 32), (T.PR[:, 0:128], ("PR", 0, 128), col(cf, 14)),
+                         (T.PR[:, 128:256], ("PR", 128, 256), col(cf, 15)), (T.PR[:, 256:384], ("PR", 256, 384), col(cf, 16))):
+        act(o, T.If[:], ["If", "cf"], [nm], 128, 1.0, ACT.Identity, scale=val)
+    ts(T.NEG[:], T.VID[:, 0:128:16], col(cf, 0), ALU.is_equal, [vid0, "cf"], ["NEG"], 8, 1.0, -128.0, ALU.mult)
+    for c in range(16):
+        ts(T.Z[:, c * ZW:c * ZW + ZW], T.VID[:, 0:ZW], col(cf, 11), ALU.is_equal, [vid0, "cf", "RM"], [("Z", c * ZW, c * ZW + ZW)],
+           ZW, 1.0, col(T.RM, c), ALU.mult)
+    ts(T.Zf[:], T.VID[:, 0:ZW], col(cf, 11), ALU.is_equal, [vid0, "cf", "RM"], ["Zf"], ZW, 1.0, col(T.RM, 0), ALU.mult)
+    fill(T.BOX[:], -4096.0, ["BOX"], 256, 0.5)
+    sel(T.BOX[:], T.BOX[:], [[0, 2], [-16, 8], [0, 16]], ALU.is_ge, 0.0, 0, 1, ["BOX"], ["BOX"], 256)
+    sel(T.BOX[:], T.BOX[:], [[0, 2], [16, 8], [0, 16]], ALU.is_ge, 0.0, 15, -1, ["BOX"], ["BOX"], 256)
+    ts(T.BO2[:], T.BOX[:, 0:256:16], -2.0, ALU.mult, ["BOX"], ["BO2"], 16)
+    ts(T.BOP[:], T.BOX[:, 0:128:16], -1.0, ALU.mult, ["BOX"], ["BOP"], 8)
+    fill(T.C2[:], -16.0, ["C2"], 64)
+    sel(T.C2[:], T.C2[:], [[0, 8], [-16, 8]], ALU.is_ge, 8192.0, 0, 1, ["C2"], ["C2"], 64)
+    sel(T.C2[:], T.C2[:], [[0, 8], [16, 8]], ALU.is_ge, 8192.0, 15, -1, ["C2"], ["C2"], 64)
+    fill(T.RST[:], 0.0, ["RST"], 256)
+    fill(T.RST[:, 0:256:16], BIG, ["RST"], 16)
+    fill(T.SC[:, 0:8], 1.0, [("SC", 0, 8)], 8)
+    fill(T.SC[:, 8:16], 32.0, [("SC", 8, 16)], 8)
+    ex = sel(T.EXP[:], T.ones[:], [[-1, 128], [0, 16]], ALU.is_equal, 0.0, 0, 1, ["ones"], ["EXP"], 2048)
+    follow(sel(T.SELU[:], T.ones[:, 0:1024], [[-16, 8], [0, 8], [-1, 16]], ALU.is_equal, 0.0, 0, 1, ["ones"], ["SELU"], 1024), sx, ss, ex)
+    follow(sel(T.E[:], T.ones[:, 0:1024], [[-16, 8], [0, 128]], ALU.is_equal, 0.0, 0, 1, ["ones"], ["E"], 1024), sx, ss, ex)
+    copy(T.SEL[:], T.E[:], ["E"], ["SEL"], 1024, 0.5)
+    fill(T.TRI[:], 4096.0, ["TRI"], 128, 0.5)
+    sel(T.TRI[:], T.TRI[:], [[-1, 128]], ALU.is_ge, 0.0, 0, 1, ["TRI"], ["TRI"], 128)
+    sel(T.U[:], T.ones[:, 0:64], [[-2, 64]], ALU.is_ge, 0.0, 0, 1, ["ones"], ["U"], 64)
+    sel(T.U[:], T.U[:], [[2, 64]], ALU.is_ge, 0.0, 1, -1, ["U"], ["U"], 64)
+
+    iota(T.W[:, 0:V], [[0, V]], OFF, [("W", 0, V)], V)
+    dma([(T.W[:, V * c:V * c + V], T.W[:, 0:V]) for c in range(1, 8)] +
+        [(T.W[:, V * c + V0:V * c + V], T.W[:, 0:V - V0]) for c in range(8, 16)], [("W", 0, V), "yBodd"],
+        [("W", V, 8 * V)] + [("W", V * c + V0, V * c + V) for c in range(8, 16)], 11.0)
+    dma([(T.W[S1, V * k:V * k + V0], T.yB[2 * k::16, 0:V0]) for k in range(8)], ["yB"], [("W", 0, 8 * V)], 1.5)
+    dma([(T.yA[:, 0:V0], T.y0[:])], [], [("yA", 0, V0)], 1.5, "G")
+
+    def search_steps(t, s):
+        have = V0 + M * t
+        xv, xn = (T.xc[:, have:have + M], "xc") if s == 0 else (T.xr[:, M * t:M * t + M], "xr")
+        st, sn = (T.st16, "st16") if s == 0 else (T.str16, "str16")
+        st = st[:, 8 * t:8 * t + 8]
+        n = dict((k, k + str(s)) for k in ("pl", "c16", "cF", "hr", "xT", "sc", "best", "low", "lowb", "sd", "ia", "im", "iF", "ih", "a", "m", "K"))
+        b = dict((k, T[v]) for k, v in n.items())
+        xw, K = T.xc[:, 0:have], b["K"]
+
+        def begin():
+            mm([(K[:, 0:128], xv, T.Ib[:], 128, False)], [xn, "Ib"], [n["K"]])
+            act(b["xT"][:], K[:, 0:128], [n["K"]], [n["xT"]], 128)
+            act(b["ia"][:], xw.indirect(st), ["xc", sn], [n["ia"]], 128, GA)
+            act(b["iF"][:], T.VID[:].indirect(st), ["VID", sn], [n["iF"]], 128, GA, ACT.Identity, bias=4112.0)
+            act(b["ih"][:], T.VID[:].indirect(st), ["VID", sn], [n["ih"]], 128, GA, ACT.Identity, bias=4096.0)
+            tt(b["im"][:], xw.indirect(st), xv, ALU.max, ["xc", xn, sn], [n["im"]], 128, GA)
+            mm([(K[:, 0:16], b["ih"][:], T.HR[:, 0:256:16], 16, False), (K[:, 0:8], b["iF"][:], T.If[:, 0:128:16], 8, True),
+                (K[:, 8:16], T.ones[:, 0:128], T.NEG[:], 8, False), (K[:, 0:16], xv, T.BOX[:, 0:256:16], 16, False),
+                (K[:, 0:16], b["ia"][:], T.BOX[:, 0:256:16], 16, False), (K[:, 0:16], b["im"][:], T.BO2[:], 16, False)],
+               [n["ih"], n["iF"], n["ia"], n["im"], xn, "HR", "If", "ones", "NEG", "BOX", "BO2"], [n["K"]])
+            copy(b["best"][:], K[:, 0:16], [n["K"]], [n["best"]], 16)
+
+        def step(h):
+            pl, pn = (st, sn) if h == 0 else (b["pl"][:], n["pl"])
+            nb = T.NBf[:, 0:have]
+            copy(b["c16"][:], T.NBi[:, 0:have].indirect(pl), [("NBi", 0, have), pn], [n["c16"]], 128, GA)
+            for q in range(4):
+                lo, vr = 512 * q, "VR%d%d" % (s, q % 2)
+                act(b["a"][:, lo:lo + 512], xw.indirect(b["c16"][:, 32 * q:32 * q + 32]), ["xc", n["c16"]], [(n["a"], lo, lo + 512)], 512, GA)
+                mm([(T[vr][:], b["xT"][:], T.EXP[:, lo:lo + 512], 512, False)], [n["xT"], "EXP"], [vr])
+                tt(b["m"][:, lo:lo + 512], b["a"][:, lo:lo + 512], T[vr][:], ALU.max, [(n["a"], lo, lo + 512), vr], [(n["m"], lo, lo + 512)], 512, 1.0)
+            act(b["hr"][:], nb.indirect(pl), ["NBf", pn], [n["hr"]], 128, GA, ACT.Identity, bias=4096.0)
+            act(b["cF"][:], nb.indirect(pl), ["NBf", pn, "cf"], [n["cF"]], 128, GA, ACT.Identity, bias=col(cf, 17 + h))
+            mm([(K[:, 0:256], b["hr"][:], T.HR[:], 256, False), (K[:, 0:128], b["cF"][:], T.If[:], 128, True),
+                (K[:, 128:256], T.ones[:, 0:128], T.PR[:, 128 * h:128 * h + 128], 128, False), (K[:, 0:256], xv, T.BOX[:], 256, False)],
+               [n["hr"], n["cF"], xn, "HR", "If", "ones", "PR", "BOX"], [n["K"]], True, False)
+            mm([(K[:, c:256:16], b["a"][:, c:2048:16], T.BOX[:, 0:256:16], 16, False) for c in range(16)], [n["a"], "BOX"], [n["K"]], False, False)
+            mm([(K[:, c:256:16], b["m"][:, c:2048:16], T.BO2[:], 16, False) for c in range(16)], [n["m"], "BO2"], [n["K"]], False, True)
+            scan(b["sc"][:], T.RST[:], K[:, 0:256], ["RST", n["K"]], [n["sc"]], 256)
+            tt(b["best"][:], b["sc"][:, 15:256:16], b["best"][:], ALU.min, [n["sc"], n["best"]], [n["best"]], 16)
+            ts(b["low"][:], b["best"][:], 63, ALU.bitwise_and, [n["best"]], [n["low"]], 16)
+            tt(b["lowb"][:], b["low"][:], T.SC[:], ALU.mult, [n["low"], "SC"], [n["lowb"]], 16)
+            mm([(K[:, 0:64], T.Ib[:], T.C2[:], 64, False)] +
+               [(K[:, 8 * u:8 * u + 8], T.SELU[:, 128 * u:128 * u + 128], b["lowb"][:, 8 * w:8 * w + 8], 8, False) for u in range(8) for w in range(2)],
+               ["Ib", "C2", "SELU", n["lowb"]], [n["K"]])
+            scan(b["sd"][:], T.RST[:, 0:128:2], K[:, 0:64], ["RST", n["K"]], [n["sd"]], 64)
+            copy(b["pl"][:], b["sd"][:, 7:64:8], [n["sd"]], [n["pl"]], 8)
+
+        return begin, step
+
+    def send_y(t):
+        have = V0 + M * t
+        src = T.ysend[:, M * t:M * t + M]
+        act(src, T.yA[:, 0:have].indirect(T.pl1[:]), [("yA", 0, have), "pl1"], [("ysend", M * t, M * t + M)], 128, GA)
+        rid, pid = topo.addr(near(t), core)
+        engs = widest(topo.engines(core, near(t)))
+        sem = T.sem["ry%d" % t]
+        sent[0] += len(engs)
+        s = add("G", lambda: [g.remote_dma(T.yA[:, have:have + M], src, sem, T.sem.sent, pid, rid, mask_of(engs))],
+                [("ysend", M * t, M * t + M)], [], 1.0, 3.0, "remote")
+        add("none", None, [], [("yA", have, have + M)], 0.0, 0.0, "recv", [s], ("ry%d" % t, len(widest(topo.engines(far(t), core)))))
+
+    def enter(t):
+        have = V0 + M * t
+        now = have + M
+        pl, nb, xw = T.pl0[:], T.NBf[:, 0:have], T.xc[:, 0:have]
+        hk = [(h, k) for h in range(2) for k in range(8)]
+        K, R = T.K0, T.VR00
+        enc = OFF - ENC * (t + 1)
+        iota(T.WENC[:], [[1, 128], [0, 8]], have + enc, ["WENC"], 1024)
+        shift(T.WL[:], T.VID[:, have:now:2], col(cf, 5), ["VID", "cf"], ["WL"], 64)
+        shift(T.WLe[:], T.WL[:], float(enc), ["WL"], ["WLe"], 64)
+        shift(T.BASE[:, 0:64], T.WL[:], col(cf, 12), ["WL", "cf"], [("BASE", 0, 64)], 64)
+        shift(T.BASE[:, 64:128], T.WL[:], col(cf, 13), ["WL", "cf"], [("BASE", 64, 128)], 64)
+        copy(T.cb[:], nb.indirect(pl), ["NBf", "pl0"], ["cb"], 128, GA)
+        mm([(R[:, 0:64], zmat(2 * ((k + 1) % 8), 8 * h + k), T.cb[:, h:128:2], 64, False) for (h, k) in hk], ["Z", "cb"], ["VR00"])
+        copy(T.CL16[:], R[:, 0:64], ["VR00"], ["CL16"], 64)
+        tt(T.P1[:, 0:64], R[:, 0:64], T.WL[:], ALU.subtract, ["VR00", "WL"], [("P1", 0, 64)], 64, 1.0)
+        copy(T.G1[:], nb.indirect(T.CL16[:]), ["NBf", "CL16"], ["G1"], 1024, GA)
+        copy(T.brep[:], T.VID[:].indirect(pl), ["VID", "pl0"], ["brep"], 128, GA)
+        ts(T.nbrep[:], T.VID[:].indirect(pl), -1.0, ALU.mult, ["VID", "pl0"], ["nbrep"], 128, GA)
+        for x in range(2):
+            vr = "VR0%d" % x
+            lst = [(T[vr][:], T.nbrep[:], T.SEL[:, 512 * x:512 * x + 512], 512, False)]
+            for q in range(4):
+                o = T[vr][:, 128 * q:128 * q + 128]
+                lst += [(o, T.SEL[:, 512 * x + 128 * q:512 * x + 128 * q + 128], T.brep[:], 128, False), (o, T.Ib[:], T.TRI[:], 128, False)]
+            mm(lst, ["nbrep", "brep", "SEL", "Ib", "TRI"], [vr])
+            ts(T.E[:, 512 * x:512 * x + 512], T[vr][:], 0.0, ALU.is_equal, [vr], [("E", 512 * x, 512 * x + 512)], 512)
+        for d in range(2):
+            mm([(K[:, 64 * d:64 * d + 64], zmat(2 * k + d, 8 * h + k), T.G1[:, 8 * h + k:1024:16], 64, False) for (h, k) in hk], ["Z", "G1"], ["K0"])
+        copy(T.FA16[:], K[:, 0:128], ["K0"], ["FA16"], 128)
+        tt(T.P1[:, 64:128], K[:, 0:64], T.WL[:], ALU.subtract, ["K0", "WL"], [("P1", 64, 128)], 64, 1.0)
+        tt(T.P2[:, 192:256], K[:, 64:128], T.WL[:], ALU.subtract, ["K0", "WL"], [("P2", 192, 256)], 64, 1.0)
+        shift(T.P1[:, 128:192], T.P1[:, 0:64], float(8 * V), [("P1", 0, 64)], [("P1", 128, 192)], 64)
+        shift(T.P1[:, 192:256], T.P2[:, 192:256], -float(8 * V), [("P2", 192, 256)], [("P1", 192, 256)], 64)
+        act(T.P2[:, 0:64], T.P1[:, 64:128], [("P1", 64, 128)], [("P2", 0, 64)], 64)
+        act(T.P2[:, 64:128], T.P1[:, 0:64], [("P1", 0, 64)], [("P2", 64, 128)], 64)
+        act(T.P2[:, 128:192], T.P1[:, 0:64], [("P1", 0, 64)], [("P2", 128, 192)], 64)
+        for d in range(2):
+            lo = 1024 * d
+            act(T.a0[:, lo:lo + 1024], xw.indirect(T.FA16[:, 64 * d:64 * d + 64]), ["xc", "FA16"], [("a0", lo, lo + 1024)], 1024, GA)
+            tt(T.m0[:, lo:lo + 1024], xw.indirect(T.CL16[:]), T.a0[:, lo:lo + 1024], ALU.max, ["xc", "CL16", ("a0", lo, lo + 1024)], [("m0", lo, lo + 1024)], 1024, GA)
+        for q in range(2):
+            vr = "VR0%d" % q
+            mm([(T[vr][:], T.xT0[:], T.EXP[:, 1024 * q:1024 * q + 1024:2], 512, False)], ["xT0", "EXP"], [vr])
+        for d in range(2):
+            for q in range(2):
+                lo, vr = 1024 * d + 512 * q, "VR0%d" % q
+                tt(T.mv[:, lo:lo + 512], T.a0[:, lo:lo + 512], T[vr][:], ALU.max, [("a0", lo, lo + 512), vr], [("mv", lo, lo + 512)], 512, 1.0)
+        neg = T.BOX[:, 0:128:16]
+        for k in range(8):
+            o = K[:, k:64:8]
+            mm([(o, T.m0[:, k:1024:8], T.BOP[:], 8, False), (o, T.mv[:, k:1024:8], neg, 8, False),
+                (o, T.m0[:, 1024 + k:2048:8], neg, 8, False), (o, T.mv[:, 1024 + k:2048:8], T.BOP[:], 8, False)],
+               ["m0", "mv", "BOX", "BOP"], ["K0"])
+        ts(T.CH[:, 0:64], K[:, 0:64], 0.0, ALU.is_ge, ["K0"], [("CH", 0, 64)], 64)
+        ts(T.CH[:, 64:128], K[:, 0:64], 0.0, ALU.is_lt, ["K0"], [("CH", 64, 128)], 64)
+        for w in range(2):
+            mm([(R[:, 64 * w:64 * w + 64], T.Ib[:], T.CH[:, 64 - 64 * w:128 - 64 * w], 64, False)] +
+               [(R[:, 64 * w + 8 * q:64 * w + 8 * q + 8], T.E[:, 128 * q:128 * q + 128], T.CH[:, 64 * w + 8 * q:64 * w + 8 * q + 8], 8, False)
+                for q in range(8)], ["Ib", "CH", "E"], ["VR00"])
+        for h in range(2):
+            ts(T.LX[:, :, h, :], R[:, 0:128], 0.0, ALU.is_equal, ["VR00", "cf"], [("LX", h, h + 1)], 128, 1.0, col(cf, 10 if h == 0 else 2), ALU.mult)
+        for q in range(4):
+            mm([(K[:, 64 * q:64 * q + 64], T.LX[:, 8 * (q // 2):8 * (q // 2) + 8, :, :], T.U[:], 64, False)], ["LX", "U"], ["K0"])
+        tt(T.t1[:], K[:, 0:256], T.P1[:], ALU.mult, ["K0", "P1"], ["t1"], 256, 1.0)
+        tt(T.s1[:], T.t1[:, 0:128], T.t1[:, 128:256], ALU.add, ["t1"], ["s1"], 128)
+        tt(T.s2[:], T.s1[:], T.BASE[:], ALU.add, ["s1", "BASE"], ["s2"], 128)
+        copy(T.O16[:], T.s2[:], ["s2"], ["O16"], 128)
+        tt(T.t2[:], K[:, 0:256], T.P2[:], ALU.mult, ["K0", "P2"], ["t2"], 256, 1.0)
+        tt(T.HT[:], T.t2[:, 0:128], T.t2[:, 128:256], ALU.add, ["t2"], ["HT"], 128)
+        act(T.W[:].indirect(T.O16[:, 0:64]), T.WENC[:], ["O16", "WENC"], ["W"], 1024, SCA, ACT.Silu)
+        tt(T.IV[:], T.W[:].indirect(T.O16[:, 64:128]), T.WENC[:], ALU.min, ["W", "O16", "WENC"], ["IV"], 1024, GA)
+        act(T.W[:].indirect(T.O16[:, 64:128]), T.IV[:], ["O16", "IV"], ["W"], 1024, SCA, ACT.Silu)
+        dma([(T.NBraw[0::2, :], T.W[S1, 0:8 * V]), (T.NBraw[1::2, :], T.W[S2, 8 * V:16 * V])], ["W"], ["NBraw"], 1.5)
+        mm([(R[:, 0:64], T.Zf[:, 15 - c:143 - c], T.IV[:, c:1024:16], 64, True) for c in range(16)], ["Zf", "IV"], ["VR00"])
+        tt(T.win[:], R[:, 0:64], T.WLe[:], ALU.is_equal, ["VR00", "WLe"], ["win"], 64, 1.0)
+        for d in range(2):
+            lo = 64 * d
+            tt(T.nw[:, lo:lo + 64], T.win[:], T.HT[:, lo:lo + 64], ALU.mult, ["win", "HT"], [("nw", lo, lo + 64)], 64)
+            tt(T.NEW[:, lo:lo + 64], T.nw[:, lo:lo + 64], T.WL[:], ALU.add, [("nw", lo, lo + 64), "WL"], [("NEW", lo, lo + 64)], 64)
+        for h in range(2):
+            mm([(K[:, h:128:2], zmat(8 * h + k, 2 * k + d), T.NEW[:, 64 * d:64 * d + 64], 64, False) for k in range(8) for d in range(2)],
+               ["Z", "NEW"], ["K0"])
+        copy(T.NBi[:, have:now], K[:, 0:128], ["K0"], [("NBi", have, now)], 128)
+        if t + 1 < RO:
+            shift(T.NWB[:], K[:, 0:128], float(OFF), ["K0"], ["NWB"], 128)
+        copy(T.NBi[:, 0:have], T.NBraw[:, 0:have], ["NBraw"], [("NBi", 0, have)], have)
+        ts(T.NBi[:, 0:have], T.NBi[:, 0:have], ENC - 1, ALU.bitwise_and, [("NBi", 0, have)], [("NBi", 0, have)], have)
+        copy(T.NB16[:, 0:now], T.NBi[:, 0:now], ["NBi"], ["NB16"], now)
+        copy(T.NBf[:, 0:now], T.NBi[:, 0:now], ["NBi"], ["NBf"], now)
+        al, bl = "AL%d" % (t % 2), "BL%d" % (t % 2)
+        dma([(T[al][:, 0:now // 2], T.NB16[0::2, 0:now]), (T[bl][:, 0:now // 2], T.NB16[1::2, 0:now])], ["NB16"], [al, bl], 0.6)
+        if t + 1 < RO:
+            dma([(T.W[S1, V * k + have:V * k + now], T.NWB[2 * k::16, :]) for k in range(8)] +
+                [(T.W[S2, V * (8 + k) + have:V * (8 + k) + now], T.NWB[2 * k + 1::16, :]) for k in range(8)], ["NWB"], ["W"], 0.5)
+        else:
+            dma([(T.nx[:], T.NBf[0::2, :])], ["NBf"], [], 1.0)
+
+    turn = [0, 0]
+
+    def sweeps(t):
+        now = V0 + M * (t + 1)
+        H = now // 2
+        al, bl = "AL%d" % (t % 2), "BL%d" % (t % 2)
+        nch, n = H // CU, 16 * CU
+        groups = [list(range(a, min(a + 4, nch - 1))) for a in range(0, nch - 1, 4)] + [[nch - 1]]
+        alone = t == RO - 1
+        for s in range(SWEEPS):
+            src, dst = ("yA", "yB") if s == 0 else ("yB", "yA")
+            yw = T[src][:, 0:now]
+            if alone and s == 0:
+                shift(T.NBraw[:], T.yA[:], 0.5, ["yA"], ["NBraw"], V, scale=0.5)
+            for grp in groups:
+                bank = "SW%d" % (turn[0] % 2)
+                turn[0] += 1
+                for q, j in enumerate(grp):
+                    ia, ip = n * (turn[1] % NBUF), n * (NBUF + turn[1] % NBUF)
+                    turn[1] += 1
+                    A, P = T.PS[:, ia:ia + n], T.PS[:, ip:ip + n]
+                    ta, tp = ("PS", ia, ia + n), ("PS", ip, ip + n)
+                    act(A, yw.indirect(T[al][:, CU * j:CU * j + CU]), [(src, 0, now), al], [ta], n, GA)
+                    tt(P, yw.indirect(T[bl][:, CU * j:CU * j + CU]), A, ALU.mult, [(src, 0, now), bl, ta], [tp], n, GA)
+                    for h in range(2):
+                        o = T[bank][:, 256 * h + CU * q:256 * h + CU * q + CU]
+                        mm(([] if alone else [(o, T.Ih[:], T[src][:, H * h + CU * j:H * h + CU * j + CU], CU, True)]) +
+                           [(o, T.In[:], T.PS[:, ip + 2 * k + h:ip + n:16], CU, True) for k in range(8)],
+                           [tp, (src, 0, now), "Ih", "In"], [bank])
+                wd, outs = CU * len(grp), []
+                for h in range(2):
+                    lo = H * h + CU * grp[0]
+                    o, ps, tk = T[dst][:, lo:lo + wd], T[bank][:, 256 * h:256 * h + wd], (dst, lo, lo + wd)
+                    if alone:
+                        tt(o, T.NBraw[:, lo:lo + wd], ps, ALU.add, [bank, ("NBraw", lo, lo + wd)], [tk], wd, 1.0)
+                        if s + 1 < SWEEPS:
+                            shift(T.NBraw[:, lo:lo + wd], o, 0.5, [tk], [("NBraw", lo, lo + wd)], wd, scale=0.5)
+                    else:
+                        shift(o, ps, 0.5, [bank], [tk], wd)
+                    outs.append(lo)
+                if t == RO - 1 and s == SWEEPS - 1:
+                    dma([(T.y[:, lo:lo + wd], T[dst][:, lo:lo + wd]) for lo in outs], [(dst, lo, lo + wd) for lo in outs], [], 0.3)
+
+    for t in range(RO):
+        parts = [search_steps(t, 0), search_steps(t, 1)]
+        for (begin, step) in parts:
+            begin()
+        for h in range(HOPS):
+            for (begin, step) in parts:
+                step(h)
+        send_y(t)
+        enter(t)
+        sweeps(t)
+    return ops, sent[0]
+
+
+def rank_program(g, core, T, topo):
+    if T.rank_of(core) is None:
+        return
+    ops, sent = build_ops(g, core, T, topo)
+    order = plan_order(ops)
+    queue = {"V": g.vector, "S": g.scalar, "P": g.tensor, "G": g, "Y": g.sync}
+    count = {"V": 0, "S": 0, "P": 0, "G": 0}
+    waited = dict((q, {}) for q in queue)
+    final, ndma = {}, [0]
+    for i in order:
+        o = ops[i]
+        if o["kind"] == "recv":
+            o["done"] = o["sem"]
+            final[o["sem"][0]] = o["sem"][1]
+            continue
+        q = queue[o["eng"]]
+        need = {}
+        for d in o["hard"]:
+            name, val = ops[d]["done"]
+            need[name] = max(need.get(name, 0), val)
+        for name in sorted(need):
+            if waited[o["eng"]].get(name, 0) < need[name]:
+                q.wait_ge(T.sem[name], need[name])
+                waited[o["eng"]][name] = need[name]
+        ins = o["fn"]()
+        if o["kind"] == "dma":
+            name = "d%d" % ndma[0]
+            ndma[0] += 1
+            for x in ins:
+                x.then_inc(T.sem[name], 16)
+            o["done"] = (name, 16 * len(ins))
+        elif o["kind"] == "remote":
+            o["done"] = ("sent", sent)
+        else:
+            name = "e" + o["eng"]
+            for x in ins:
+                x.then_inc(T.sem[name], 1)
+            count[o["eng"]] += len(ins)
+            o["done"] = (name, count[o["eng"]])
+        final[o["done"][0]] = max(final.get(o["done"][0], 0), o["done"][1])
+    for name in sorted(final):
+        if waited["G"].get(name, 0) < final[name]:
+            g.wait_ge(T.sem[name], final[name])

@@ -3,12 +3,25 @@ from concourse.mybir import AluOpType as ALU, ActivationFunctionType as ACT
 
 N, V0, M, RO, HOPS, SWEEPS = 4, 1024, 128, 3, 3, 2
 V = V0 + RO * M
+PAD = 32
+U, OLD = PAD + V, PAD + RO * M
 F32, BF, I32, U16, F16 = "float32", "bfloat16", "int32", "uint16", "float16"
 ZW = 144
-CU = 64
-NBUF = 3
-ENC, OFF = 4096, 16384
+QM = V // 4
+RING = 7168
 BIG = 33554432.0
+NONE = 2048
+CHUNKS = [[48] * 6, [40] * 8, [24, 40, 48, 48, 48, 40, 48, 32, 24]]
+SCANS = [[], [], [(7, 0), (7, 1), (8, 0), (8, 1)]]
+SWEEP_BANKS = [["SW0", "SW1", "VR10"], ["SW0", "SW1", "VR10"], ["SW0", "SW1", "VR10", "VR11", "K1", "K0"]]
+ON_VECTOR = [[2, 2], [2, 3], [2, 3]]
+MIXED = [[0, 0], [0, 0], [0, 0]]
+BY_DMA = [[0, 1, 2, 3, 4], [0, 1, 2, 3, 4, 5, 6], [0, 2, 4, 5]]
+HALVES = [2, 1, 1]
+SCATTERS = ["SVVS", "SS", "SS"]
+EVAC = ["S", "S", "S"]
+EARLY = [0, 0, 3]
+INV_SPLIT = 14
 
 
 def sb(w, d):
@@ -16,70 +29,141 @@ def sb(w, d):
 
 
 SCRATCH = {
-    "W": sb(16 * V, F32), "PS": sb(2 * NBUF * 16 * CU, F32), "mv": sb(2048, BF), "NWB": sb(128, F32), "yA": sb(V, F32), "yB": sb(V, F32),
-    "NBraw": sb(V, F32), "NBi": sb(V, I32), "NBf": sb(V, F32), "NB16": sb(V, U16),
-    "AL0": sb(V // 2, U16), "AL1": sb(V // 2, U16), "BL0": sb(V // 2, U16), "BL1": sb(V // 2, U16),
-    "VID": sb(V, F32), "xc": sb(V, BF), "xr": sb(RO * M, BF),
+    "W": sb(16 * V, F32), "PS": sb(RING, F32), "mv": sb(2048, BF), "yA": sb(U, F32), "yB": sb(U, F32),
+    "NB0": sb(U, F32), "NB1": sb(U, F32), "NBi": sb(V0, I32), "NB16": sb(V, U16), "LS0": sb(4 * QM, U16), "LS1": sb(4 * QM, U16),
+    "VID": sb(U, F32), "xc": sb(U, BF), "xr": sb(RO * M, BF),
     "sti": sb(24, I32), "st16": sb(24, U16), "str16": sb(24, U16),
     "Lraw": sb(512, I32), "L16": sb(512, U16), "IV": sb(V0, F32), "WENC": sb(V0, F32),
-    "a0": sb(2048, BF), "a1": sb(2048, BF), "m0": sb(2048, BF), "m1": sb(2048, BF),
-    "ones": sb(2048, BF), "EXP": sb(2048, BF), "SELU": sb(1024, BF), "SEL": sb(1024, F16),
+    "d0": sb(2048, BF), "d1": sb(2048, BF), "r0": sb(2048, BF), "r1": sb(2048, BF), "ve0": sb(2048, BF), "ve1": sb(2048, BF),
+    "ones": sb(1024, BF), "SELU": sb(1024, BF), "SEL": sb(1024, F16),
     "Z": sb(16 * ZW, F16), "Zf": sb(ZW, F32), "RM": sb(16, F32),
-    "Ib": sb(128, BF), "If": sb(128, F32), "Ih": sb(128, F32), "In": sb(128, F32),
-    "HR": sb(256, BF), "PR": sb(384, BF), "NEG": sb(8, BF), "BOX": sb(256, BF), "BO2": sb(16, BF), "BOP": sb(8, BF),
-    "C2": sb(64, BF), "RST": sb(256, F32), "SC": sb(16, F32), "TRI": sb(128, BF), "U": sb(64, BF),
-    "ci": sb(16, I32), "cf": sb(24, F32), "WL": sb(64, F32), "WLe": sb(64, F32), "BASE": sb(128, F32),
+    "Ib": sb(128, BF), "If": sb(128, F32), "Ih": sb(128, F32), "In": sb(128, F32), "I16": sb(128, F16),
+    "HR": sb(256, BF), "PR": sb(384, BF), "NEG": sb(8, BF), "BOX": sb(16, BF), "BO2": sb(16, BF), "BOP": sb(8, BF),
+    "C2": sb(64, BF), "ZERO": sb(64, BF), "RST": sb(256, F32), "SC": sb(16, F32), "TRI": sb(128, BF),
+    "UU1": sb(256, BF), "UU2": sb(128, BF), "MJ1": sb(2, F32), "MJ2": sb(4, F32), "ci": sb(16, I32), "cf": sb(28, F32), "WL": sb(64, F32), "BASE": sb(128, F32),
     "G1": sb(1024, F16), "E": sb(1024, BF), "cb": sb(128, F16), "brep": sb(128, F16), "nbrep": sb(128, F16),
-    "CL16": sb(64, U16), "FA16": sb(128, U16), "CH": sb(128, BF), "LX": sb([16, 2, 8], BF),
-    "P1": sb(256, F32), "P2": sb(256, F32), "t1": sb(256, F32), "t2": sb(256, F32), "s1": sb(128, F32), "s2": sb(128, F32),
+    "CL16": sb(64, U16), "FA16": sb(128, U16), "CH": sb(128, BF), "LX1": sb([16, 2, 8], BF), "LX2": sb([32, 4, 4], BF),
+    "P1": sb(256, F32), "t1": sb(256, F32), "s1": sb(128, F32), "s2": sb(128, F32),
     "HT": sb(128, F32), "O16": sb(128, U16), "win": sb(64, F32), "nw": sb(128, F32), "NEW": sb(128, F16),
     "ysend": sb(RO * M, F32),
 }
 for _s in "01":
     SCRATCH.update({"pl" + _s: sb(8, U16), "c16" + _s: sb(128, U16), "cF" + _s: sb(128, F32), "hr" + _s: sb(128, BF),
-                    "xT" + _s: sb(128, BF), "sc" + _s: sb(256, F32), "best" + _s: sb(16, I32),
+                    "sc" + _s: sb(256, F32), "best" + _s: sb(16, I32),
                     "low" + _s: sb(16, I32), "lowb" + _s: sb(16, BF), "sd" + _s: sb(64, F32),
                     "ia" + _s: sb(128, BF), "im" + _s: sb(128, BF), "iF" + _s: sb(128, F32), "ih" + _s: sb(128, BF)})
 BANKS = ["SW0", "SW1", "VR00", "VR01", "VR10", "VR11", "K0", "K1"]
 for _b in BANKS:
     SCRATCH[_b] = ("psum", [128, 512], F32)
-NDMA = 40
+NDMA = 120
 SEMAPHORES = ["eV", "eS", "eP", "eG", "sent", "rx", "rst", "ry0", "ry1", "ry2"] + ["d%d" % i for i in range(NDMA)]
 
-CYC, GA, SCA, PEC, SYNC = 1.0e-3, 1.6, 3.8, 0.5e-3, 0.12
+FIG = {"cyc": 0.83e-3, "ga": 1.56, "sca": 3.8, "pe": 0.43e-3, "sync": 0.1, "issue": 0.06, "issue_g": 1.0, "land": 2.0, "unit": 235.0}
+FIGS = [FIG, dict(FIG, ga=1.2, sca=2.5, pe=0.5e-3), dict(FIG, cyc=1.0e-3, ga=1.95, sca=5.0, pe=0.5e-3, unit=320.0),
+        dict(FIG, sync=0.18, issue=0.15, issue_g=1.5, land=3.0, unit=260.0)]
+LOOKS, PASSES, MOVES, SLACK, SEED = (0.1, 0.2, 0.3, 0.45), 4, 1500, 0.002, 3
+PLAN = {}
 
 
-def plan_order(ops):
+def first_new(t):
+    return OLD - M * (t + 1)
+
+
+def lay_out(ops, rank, look, after):
     n = len(ops)
-    succ = [[] for _ in range(n)]
-    for i, o in enumerate(ops):
-        for d in o["deps"]:
-            succ[d].append(i)
-    prio = [0.0] * n
-    for i in range(n - 1, -1, -1):
-        prio[i] = ops[i]["cost"] + ops[i]["lat"] + max([prio[j] + SYNC for j in succ[i]] + [0.0])
-    left = [len(o["deps"]) for o in ops]
-    rdy = [0.0] * n
-    ready = [i for i in range(n) if left[i] == 0]
-    free, order = {}, []
-    while ready:
-        est = dict((i, max(rdy[i], free.get(ops[i]["eng"], 0.0))) for i in ready)
-        first = min(ready, key=lambda i: (est[i], -prio[i]))
-        eng = ops[first]["eng"]
-        near = [i for i in ready if ops[i]["eng"] == eng and est[i] <= est[first] + 0.3]
-        i = max(near, key=lambda j: (prio[j], -j))
-        ready.remove(i)
+    left, rdy, at = [0] * n, [0.0] * n, [0.0] * n
+    for i in range(n):
+        for (j, gap) in after[i]:
+            left[j] += 1
+    ready = dict((e, []) for e in ("V", "S", "P", "G", "Y", "none"))
+    free = dict((e, 0.0) for e in ready)
+    for i in range(n):
+        if not left[i]:
+            ready[ops[i]["eng"]].append(i)
+    order = []
+    while len(order) < n:
+        t, e = min((max(free[e], min(rdy[i] for i in l)), e) for e, l in ready.items() if l)
+        i = max((j for j in ready[e] if rdy[j] <= t + look), key=lambda j: (rank[j], -j))
+        ready[e].remove(i)
         order.append(i)
-        ops[i]["at"] = est[i]
-        if eng != "none":
-            free[eng] = est[i] + ops[i]["cost"]
-        done = est[i] + ops[i]["cost"] + ops[i]["lat"]
-        for j in succ[i]:
-            rdy[j] = max(rdy[j], done + SYNC)
+        at[i] = max(t, rdy[i])
+        if e != "none":
+            free[e] = at[i] + ops[i]["cost"]
+        for (j, gap) in after[i]:
+            rdy[j] = max(rdy[j], at[i] + ops[i]["cost"] + gap)
             left[j] -= 1
-            if left[j] == 0:
-                ready.append(j)
-    return order
+            if not left[j]:
+                ready[ops[j]["eng"]].append(j)
+    return max(at[i] + ops[i]["cost"] + ops[i]["lat"] for i in range(n)), order, at
+
+
+def links(ops, fig):
+    succ, pred = [[] for _ in ops], [[] for _ in ops]
+    for j, o in enumerate(ops):
+        for i in sorted(o["deps"]):
+            gap = ops[i]["lat"] + (0.0 if i not in o["hard"] else fig["sync"] / 2 if ops[i]["eng"] == o["eng"] else fig["sync"])
+            succ[i].append((j, gap))
+            pred[j].append((i, gap))
+    return succ, pred
+
+
+def length(ops, pred, order):
+    free, end, last = {}, [0.0] * len(ops), 0.0
+    for i in order:
+        o = ops[i]
+        t = free.get(o["eng"], 0.0)
+        for (j, gap) in pred[i]:
+            if end[j] + gap > t:
+                t = end[j] + gap
+        end[i] = t + o["cost"]
+        if o["eng"] != "none":
+            free[o["eng"]] = end[i]
+        last = max(last, end[i] + o["lat"])
+    return last
+
+
+def plan_order(builds):
+    ops = builds[0]
+    n = len(ops)
+    succ, pred = links(ops, FIGS[0])
+    preds = [links(b, f)[1] for (b, f) in zip(builds, FIGS)]
+
+    def again(plan, look):
+        back = lay_out(ops, [plan[2][i] + ops[i]["cost"] for i in range(n)], look, pred)[2]
+        return lay_out(ops, [back[i] + ops[i]["cost"] for i in range(n)], look, succ)
+
+    def score(plan):
+        return sum(length(b, p, plan[1]) / f["unit"] for (b, p, f) in zip(builds, preds, FIGS))
+
+    way = [0.0] * n
+    for i in range(n - 1, -1, -1):
+        way[i] = ops[i]["cost"] + max([way[j] + gap for (j, gap) in succ[i]] + [ops[i]["lat"]])
+    plans = []
+    for look in LOOKS:
+        plans.append(lay_out(ops, way, look, succ))
+        for _ in range(PASSES):
+            plans.append(again(plans[-1], look))
+    cur = min(plans, key=score)
+    now = least = score(cur)
+    best, parts, seed = cur, sorted(set(o["part"] for o in ops)), [SEED]
+
+    def draw():
+        seed[0] = (seed[0] * 1103515245 + 12345) % 2147483648
+        return seed[0] / 2147483648
+
+    for _ in range(MOVES):
+        lo = draw() * cur[0]
+        hi, part, by, look = lo + 5 + 35 * draw(), parts[int(draw() * len(parts))], 12 * (draw() - 0.5), 0.1 + 0.3 * draw()
+        at = cur[2]
+        plan = lay_out(ops, [0.4 * draw() - at[i] + (by if lo <= at[i] < hi and ops[i]["part"] == part else 0.0) for i in range(n)], look, succ)
+        if draw() < 0.3:
+            plan = again(plan, look)
+        s = score(plan)
+        if s <= now + SLACK:
+            cur, now = plan, s
+        if s < least:
+            best, least = plan, s
+    return best
 
 
 def mask_of(engs):
@@ -96,9 +180,10 @@ def widest(engs):
     return engs[:n]
 
 
-def build_ops(g, core, T, topo):
+def build_ops(g, core, T, topo, fig):
     rank = T.rank_of(core)
-    ops, wr_of, rd_of = [], {}, {}
+    CYC, GA, SCA, PEC = fig["cyc"], fig["ga"], fig["sca"], fig["pe"]
+    ops, wr_of, rd_of, part = [], {}, {}, ["setup"]
     ALL = 1 << 30
 
     def tok(x):
@@ -124,7 +209,7 @@ def build_ops(g, core, T, topo):
         for (b, lo, hi) in reads:
             rd_of.setdefault(b, []).append((i, lo, hi))
         ops.append({"eng": eng, "fn": fn, "deps": deps, "hard": hard, "cost": cost, "lat": lat, "kind": kind, "sem": sem,
-                    "w": [x[0] for x in writes][:2]})
+                    "w": writes[0][0] if writes else "", "part": part[0]})
         return i
 
     def follow(i, *earlier):
@@ -133,10 +218,10 @@ def build_ops(g, core, T, topo):
     vq, sq, pq = g.vector, g.scalar, g.tensor
 
     def vec(fn, r, w, n, per=1.0):
-        return add("V", lambda: [fn()], r, w, 0.06 + max(64, n * per) * CYC)
+        return add("V", lambda: [fn()], r, w, 0.05 + max(16, n * per) * CYC)
 
     def act(out, in_, r, w, n, per=1.0, func=ACT.Copy, **kw):
-        return add("S", lambda: [sq.activation(out, in_, func, **kw)], r, w, 0.08 + max(64, n * per) * CYC)
+        return add("S", lambda: [sq.activation(out, in_, func, **kw)], r, w, 0.065 + max(16, n * per) * CYC)
 
     def pool(fn, r, w, n):
         return add("G", lambda: [fn()], r, w, 0.17 + 2 * n * CYC)
@@ -148,11 +233,11 @@ def build_ops(g, core, T, topo):
         cost = sum(max(64, x[3]) * PEC * (4 if x[4] else 1) for x in lst)
         last = len(lst) - 1
         return add("P", lambda: [pq.matmul(x[0], x[1], x[2], start and n == 0, stop and n == last) for n, x in enumerate(lst)],
-                   r, w, cost + 0.05)
+                   r, w, cost + 0.01)
 
-    def dma(pairs, r, w, us, q="Y"):
+    def dma(pairs, r, w, us, q="Y", **kw):
         eq = {"Y": g.sync, "S": sq, "G": g}[q]
-        return add(q, lambda: [eq.dma_start(o, i) for (o, i) in pairs], r, w, (0.1 if q != "G" else 1.0) * len(pairs), 2.0 + us, "dma")
+        return add(q, lambda: [eq.dma_start(o, i, **kw) for (o, i) in pairs], r, w, fig["issue_g" if q == "G" else "issue"] * len(pairs), fig["land"] + us, "dma")
 
     def copy(out, in_, r, w, n, per=1.0):
         return vec(lambda: vq.tensor_copy(out, in_), r, w, n, per)
@@ -182,39 +267,52 @@ def build_ops(g, core, T, topo):
         return T.Z[:, o:o + 128]
 
     S1, S2 = slice(0, 128, 18), slice(14, 113, 14)
+    WO = OLD - PAD
+    minus = T.HR[:, 0:128]
 
     dma([(T.Lraw[:, 64 * k:64 * k + 64], T.nx0[k::8, :]) for k in range(4, 8)], [], [("Lraw", 256, 512)], 0.3)
     dma([(T.Lraw[:, 64 * k:64 * k + 64], T.nx0[k::8, :]) for k in range(4)], [], [("Lraw", 0, 256)], 0.3, "S")
-    dma([(T.m1[:, 0:V], T.x[:]), (T.sti[:], T.st[:])], [], ["m1", "sti"], 0.7)
-    dma([(T.NBi[0::2, 0:V0], T.nx0[:]), (T.NBi[1::2, 0:V0], T.nx0[:])], [], [("NBi", 0, V0)], 1.0)
+    dma([(T.xc[:, first_new(t):first_new(t) + M], T.x[:, V0 + M * t:V0 + M * t + M]) for t in range(RO)] + [(T.sti[:], T.st[:])],
+        [], [("xc", PAD, OLD), "sti"], 0.3)
+    dma([(T.xc[:, OLD:U], T.x[:, 0:V0])], [], [("xc", OLD, U)], 0.7)
+    dma([(T.NBi[0::2, :], T.nx0[:]), (T.NBi[1::2, :], T.nx0[:])], [], ["NBi"], 1.0)
+    fill(T.xc[:, 0:PAD], 0.0, [("xc", 0, PAD)], PAD)
+    fill(T.NB0[:, 0:OLD], 0.0, [("NB0", 0, OLD)], OLD)
+    fill(T.NB1[:, 0:PAD], 0.0, [("NB1", 0, PAD)], PAD)
 
-    early = [ts(T.xc[:], T.m1[:, 0:V], -127.0, ALU.add, ["m1"], ["xc"], V, 0.5),
-             copy(T.st16[:], T.sti[:], ["sti"], ["st16"], 24),
-             ts(T.yB[:, 0:V0], T.NBi[:, 0:V0], float(OFF), ALU.add, [("NBi", 0, V0)], ["yB", "yBodd"], V0)]
+    early = [copy(T.st16[:], T.sti[:], ["sti"], ["st16"], 24),
+             ts(T.NB0[:, OLD:U], T.NBi[:], float(OLD), ALU.add, ["NBi"], [("NB0", OLD, U), "NB0b"], V0)]
 
-    iota(T.IV[:], [[1, 64], [64, 16]], OFF, ["IV"], V0)
+    iota(T.IV[:], [[1, 64], [64, 16]], OLD, ["IV"], V0)
     for h in range(2):
         c = ("Lraw", 256 * h, 256 * h + 256)
         copy(T.L16[:, c[1]:c[2]], T.Lraw[:, c[1]:c[2]], [c], [("L16", c[1], c[2])], 256)
 
-    def invert(k, a, b, on_scalar):
-        lo = V * (8 + k)
-        win = T.W[:, lo:lo + V0].indirect(T.L16[:, 64 * k + a:64 * k + b])
-        r, w = ["IV", ("L16", 64 * k, 64 * k + 64)], [("W", lo, lo + V0)]
-        if on_scalar:
-            return act(win, T.IV[:, 16 * a:16 * b], r, w, 16 * (b - a), SCA, ACT.Silu)
-        return copy(win, T.IV[:, 16 * a:16 * b], r, w, 16 * (b - a), SCA)
+    def slot(k, d):
+        return 8 * (k % 2) + 4 * d + k // 2
 
-    invert(4, 20, 64, False)
+    def scatter(out, in_, r, w, n, q):
+        if q == "S":
+            return act(out, in_, r, w, n, SCA, ACT.Silu)
+        return copy(out, in_, r, w, n, SCA)
+
+    def invert(k, a, b, q):
+        lo = V * slot(k, 1) + WO
+        return scatter(T.W[:, lo:lo + V0].indirect(T.L16[:, 64 * k + a:64 * k + b]), T.IV[:, 16 * a:16 * b],
+                       ["IV", ("L16", 64 * k, 64 * k + 64)], [("W", lo, lo + V0)], 16 * (b - a), q)
+
+    fill(T.ones[:], 1.0, ["ones"], 1024, 0.5)
+    none = act(T.W[:, 0:WO], T.ones[:, 0:WO], ["ones"], [("W", 0, WO)], WO + 1600, 1.0, ACT.Silu, scale=float(NONE))
+    invert(4, INV_SPLIT, 64, "V")
     for k in (5, 6, 7):
-        follow(invert(k, 0, 64, False), *early)
-    last = [invert(k, 0, 64, True) for k in range(4)]
-    follow(invert(4, 0, 20, True), *last)
+        follow(invert(k, 0, 64, "V"), *early)
+    last = [invert(k, 0, 64, "S") for k in range(4)]
+    for i in last:
+        follow(i, none)
+    follow(invert(4, 0, INV_SPLIT, "S"), *last)
     for k in range(8):
-        lo = V * (8 + k)
-        dma([(T.yB[2 * k + 1::16, 0:V0], T.W[S2, lo:lo + V0])], [("W", lo, lo + V0)], [("yBodd", k, k + 1)], 0.3)
-    ts(T.NBi[:, 0:V0], T.yB[:, 0:V0], -float(OFF), ALU.add, ["yB", "yBodd"], [("NBi", 0, V0)], V0)
-    copy(T.NBf[:, 0:V0], T.NBi[:, 0:V0], [("NBi", 0, V0)], ["NBf"], V0)
+        lo = V * slot(k, 1) + WO
+        dma([(T.NB0[2 * k + 1::16, OLD:U], T.W[S2, lo:lo + V0])], [("W", lo, lo + V0)], [("NB0b", OLD + k, OLD + k + 1)], 0.2)
 
     sent = [0]
 
@@ -224,19 +322,20 @@ def build_ops(g, core, T, topo):
     def near(t):
         return T.cores[(rank - 1 - t) % N]
 
-    def fused(src, off, dst, width, sem):
+    def fused(src, offs, dst, width, sem):
         trs = []
         for t in range(RO):
             rid, pid = topo.addr(far(t), core)
             engs = topo.engines(core, far(t))[2 * t:2 * t + 2]
             trs.append(RemoteDMATransfer(dst_ids=[DstId(rid=rid, pnc=pid)], dma_engine_mask=mask_of(engs), remote_sem=sem,
-                                         src=src[:, off + width * t:off + width * t + width], dst=dst[:, width * t:width * t + width]))
+                                         src=src[:, offs[t]:offs[t] + width], dst=dst[:, width * t:width * t + width]))
         sent[0] += 2 * RO
         return lambda: [g.remote_dma_fused(trs, local_sem=T.sem.sent)]
 
-    sx = add("G", fused(T.xc, V0, T.xr, M, T.sem.rx), ["xc"], [], 2.0, 4.0, "remote")
+    sx = add("G", fused(T.xc, [first_new(t) for t in range(RO)], T.xr, M, T.sem.rx), [("xc", PAD, OLD)], [], 3.0, 4.0, "remote")
     add("none", None, [], ["xr"], 0.0, 0.0, "recv", [sx], ("rx", 2 * RO))
-    ss = add("G", fused(T.st16, 0, T.str16, 8, T.sem.rst), ["st16"], [], 1.0, 4.0, "remote")
+    ss = add("G", fused(T.st16, [8 * t for t in range(RO)], T.str16, 8, T.sem.rst), ["st16"], [], 1.0, 3.0, "remote")
+    follow(ss, sx)
     add("none", None, [], ["str16"], 0.0, 0.0, "recv", [ss], ("rst", 2 * RO))
 
     ci, cf = T.ci, T.cf
@@ -247,42 +346,47 @@ def build_ops(g, core, T, topo):
     pool(lambda: g.iota(col(ci, 0), [[0, 1]], 0, 1), [], [("ci", 0, 1)], 1)
     vid0 = ("VID", 0, ZW)
     iota(T.VID[:, 0:ZW], [[1, ZW]], 0, [vid0], ZW)
-    iota(T.VID[:, ZW:V], [[1, V - ZW]], ZW, [("VID", ZW, V)], V - ZW)
-    fill(T.ones[:], 1.0, ["ones"], 2048, 0.5)
+    iota(T.VID[:, ZW:U], [[1, U - ZW]], ZW, [("VID", ZW, U)], U - ZW)
     p = [("ci", 0, 1)]
     ts(col(ci, 1), col(ci, 0), 15, ALU.bitwise_and, p, [("ci", 1, 2)], 1)
     ts(col(ci, 2), col(ci, 0), 1, ALU.bitwise_and, p, [("ci", 2, 3)], 1)
     ts(col(ci, 3), col(ci, 0), 1, ALU.logical_shift_right, p, [("ci", 3, 4)], 1, 1.0, 7, ALU.bitwise_and)
-    ts(col(ci, 4), col(ci, 0), 7, ALU.bitwise_and, p, [("ci", 4, 5)], 1)
+    ts(col(ci, 4), col(ci, 0), 1, ALU.logical_shift_right, p, [("ci", 4, 5)], 1, 1.0, 3, ALU.bitwise_and)
     ts(col(ci, 5), col(ci, 0), 3, ALU.logical_shift_right, p, [("ci", 5, 6)], 1, 1.0, 1, ALU.bitwise_and)
     ts(col(ci, 6), col(ci, 0), 112, ALU.bitwise_and, p, [("ci", 6, 7)], 1)
+    ts(col(ci, 8), col(ci, 0), 2, ALU.logical_shift_right, p, [("ci", 8, 9)], 1, 1.0, 3, ALU.bitwise_and)
+    ts(col(ci, 9), col(ci, 0), 3, ALU.bitwise_and, p, [("ci", 9, 10)], 1)
     copy(cf[:, 0:7], ci[:, 0:7], ["ci"], [("cf", 0, 7)], 7)
-    c0 = [("cf", 0, 7)]
-    ts(col(cf, 7), col(cf, 2), 8.0, ALU.mult, c0, [("cf", 7, 8)], 1, 1.0, col(cf, 3), ALU.add)
+    copy(cf[:, 8:10], ci[:, 8:10], ["ci"], [("cf", 8, 10)], 2)
+    c0 = [("cf", 0, 10)]
+    ts(col(cf, 7), col(cf, 2), 8.0, ALU.mult, [("cf", 0, 7)], [("cf", 7, 8)], 1, 1.0, col(cf, 3), ALU.add)
     for h in range(HOPS):
         ts(col(cf, 14 + h), col(cf, 7), 64.0, ALU.mult, [("cf", 7, 8)], [("cf", 14 + h, 15 + h)], 1, 1.0, 64.0 * (16 * h + 1) - 128.0, ALU.add)
         ts(col(cf, 17 + h), col(cf, 7), 64.0, ALU.mult, [("cf", 7, 8)], [("cf", 17 + h, 18 + h)], 1, 1.0, 64.0 * (16 * h + 1) + 4112.0, ALU.add)
-    ts(col(cf, 10), col(cf, 2), -1.0, ALU.mult, c0, [("cf", 10, 11)], 1, 1.0, 1.0, ALU.add)
     ts(col(cf, 11), col(cf, 6), 15.0, ALU.add, c0, [("cf", 11, 12)], 1)
-    ts(col(cf, 12), col(cf, 4), float(V), ALU.mult, c0, [("cf", 12, 13)], 1)
-    ts(col(cf, 13), col(cf, 4), float(V), ALU.mult, c0, [("cf", 13, 14)], 1, 1.0, float(8 * V), ALU.add)
+    ts(col(cf, 10), col(cf, 2), 8.0, ALU.mult, c0, [("cf", 10, 11)], 1, 1.0, col(cf, 4), ALU.add)
+    for (cj, jj, sl) in ((20, 5, 10), (23, 8, 9)):
+        copy(col(cf, cj), col(cf, jj), c0, [("cf", cj, cj + 1)], 1)
+        for d in range(2):
+            ts(col(cf, cj + 1 + d), col(cf, sl), float(V), ALU.mult, [("cf", 0, 11)], [("cf", cj + 1 + d, cj + 2 + d)], 1, 1.0, 4 * V * d + 0.25 - PAD, ALU.add)
     ts(T.RM[:], T.VID[:, 0:16], col(cf, 1), ALU.is_equal, [vid0, ("cf", 0, 7)], ["RM"], 16)
-    ts(T.Ib[:], T.VID[:, 0:128], col(cf, 0), ALU.is_equal, [vid0, ("cf", 0, 7)], ["Ib"], 128)
-    ts(T.If[:], T.VID[:, 0:128], col(cf, 0), ALU.is_equal, [vid0, ("cf", 0, 7)], ["If"], 128)
+    for nm in ("Ib", "If", "I16"):
+        ts(T[nm][:], T.VID[:, 0:128], col(cf, 0), ALU.is_equal, [vid0, ("cf", 0, 7)], [nm], 128)
     for (o, nm, val) in ((T.Ih[:], "Ih", 0.5), (T.In[:], "In", -0.0625), (T.HR[:, 0:128], ("HR", 0, 128), -1.0),
                          (T.HR[:, 128:256], ("HR", 128, 256), 1.0 / 32), (T.PR[:, 0:128], ("PR", 0, 128), col(cf, 14)),
                          (T.PR[:, 128:256], ("PR", 128, 256), col(cf, 15)), (T.PR[:, 256:384], ("PR", 256, 384), col(cf, 16))):
-        act(o, T.If[:], ["If", "cf"], [nm], 128, 1.0, ACT.Identity, scale=val)
+        ts(o, T.If[:], val, ALU.mult, ["If", "cf"], [nm], 128)
     ts(T.NEG[:], T.VID[:, 0:128:16], col(cf, 0), ALU.is_equal, [vid0, "cf"], ["NEG"], 8, 1.0, -128.0, ALU.mult)
     for c in range(16):
         ts(T.Z[:, c * ZW:c * ZW + ZW], T.VID[:, 0:ZW], col(cf, 11), ALU.is_equal, [vid0, "cf", "RM"], [("Z", c * ZW, c * ZW + ZW)],
            ZW, 1.0, col(T.RM, c), ALU.mult)
     ts(T.Zf[:], T.VID[:, 0:ZW], col(cf, 11), ALU.is_equal, [vid0, "cf", "RM"], ["Zf"], ZW, 1.0, col(T.RM, 0), ALU.mult)
-    fill(T.BOX[:], -4096.0, ["BOX"], 256, 0.5)
-    sel(T.BOX[:], T.BOX[:], [[0, 2], [-16, 8], [0, 16]], ALU.is_ge, 0.0, 0, 1, ["BOX"], ["BOX"], 256)
-    sel(T.BOX[:], T.BOX[:], [[0, 2], [16, 8], [0, 16]], ALU.is_ge, 0.0, 15, -1, ["BOX"], ["BOX"], 256)
-    ts(T.BO2[:], T.BOX[:, 0:256:16], -2.0, ALU.mult, ["BOX"], ["BO2"], 16)
-    ts(T.BOP[:], T.BOX[:, 0:128:16], -1.0, ALU.mult, ["BOX"], ["BOP"], 8)
+    fill(T.BOX[:], -4096.0, ["BOX"], 16)
+    sel(T.BOX[:], T.BOX[:], [[0, 2], [-16, 8]], ALU.is_ge, 0.0, 0, 1, ["BOX"], ["BOX"], 16)
+    sel(T.BOX[:], T.BOX[:], [[0, 2], [16, 8]], ALU.is_ge, 0.0, 15, -1, ["BOX"], ["BOX"], 16)
+    ts(T.BO2[:], T.BOX[:], -2.0, ALU.mult, ["BOX"], ["BO2"], 16)
+    ts(T.BOP[:], T.BOX[:, 0:8], -1.0, ALU.mult, ["BOX"], ["BOP"], 8)
+    fill(T.ZERO[:], 0.0, ["ZERO"], 64)
     fill(T.C2[:], -16.0, ["C2"], 64)
     sel(T.C2[:], T.C2[:], [[0, 8], [-16, 8]], ALU.is_ge, 8192.0, 0, 1, ["C2"], ["C2"], 64)
     sel(T.C2[:], T.C2[:], [[0, 8], [16, 8]], ALU.is_ge, 8192.0, 15, -1, ["C2"], ["C2"], 64)
@@ -290,60 +394,84 @@ def build_ops(g, core, T, topo):
     fill(T.RST[:, 0:256:16], BIG, ["RST"], 16)
     fill(T.SC[:, 0:8], 1.0, [("SC", 0, 8)], 8)
     fill(T.SC[:, 8:16], 32.0, [("SC", 8, 16)], 8)
-    ex = sel(T.EXP[:], T.ones[:], [[-1, 128], [0, 16]], ALU.is_equal, 0.0, 0, 1, ["ones"], ["EXP"], 2048)
-    follow(sel(T.SELU[:], T.ones[:, 0:1024], [[-16, 8], [0, 8], [-1, 16]], ALU.is_equal, 0.0, 0, 1, ["ones"], ["SELU"], 1024), sx, ss, ex)
-    follow(sel(T.E[:], T.ones[:, 0:1024], [[-16, 8], [0, 128]], ALU.is_equal, 0.0, 0, 1, ["ones"], ["E"], 1024), sx, ss, ex)
+    sel(T.SELU[:], T.ones[:], [[-16, 8], [0, 8], [-1, 16]], ALU.is_equal, 0.0, 0, 1, ["ones"], ["SELU"], 1024)
+    sel(T.E[:], T.ones[:], [[-16, 8], [0, 128]], ALU.is_equal, 0.0, 0, 1, ["ones"], ["E"], 1024)
     copy(T.SEL[:], T.E[:], ["E"], ["SEL"], 1024, 0.5)
     fill(T.TRI[:], 4096.0, ["TRI"], 128, 0.5)
     sel(T.TRI[:], T.TRI[:], [[-1, 128]], ALU.is_ge, 0.0, 0, 1, ["TRI"], ["TRI"], 128)
-    sel(T.U[:], T.ones[:, 0:64], [[-2, 64]], ALU.is_ge, 0.0, 0, 1, ["ones"], ["U"], 64)
-    sel(T.U[:], T.U[:], [[2, 64]], ALU.is_ge, 0.0, 1, -1, ["U"], ["U"], 64)
+    for hv in sorted(set(HALVES)):
+        uu, jj, uw = "UU%d" % hv, 2 * hv, 64 // hv
+        sel(T[uu][:, 0:2 * uw], T.ones[:, 0:2 * uw], [[0, 2], [-jj, uw]], ALU.is_ge, 0.0, 0, 1, ["ones"], [(uu, 0, 2 * uw)], 2 * uw)
+        sel(T[uu][:, 0:2 * uw], T[uu][:, 0:2 * uw], [[0, 2], [jj, uw]], ALU.is_ge, 0.0, jj - 1, -1, [(uu, 0, 2 * uw)], [(uu, 0, 2 * uw)], 2 * uw)
+        for d in range(2):
+            ts(T[uu][:, (2 + d) * uw:(3 + d) * uw], T[uu][:, 0:uw], 4.0 * V * (1 - 2 * d), ALU.mult, [(uu, 0, 2 * uw)], [(uu, (2 + d) * uw, (3 + d) * uw)], uw, 0.5)
+        ts(T["MJ%d" % hv][:], T.VID[:, 0:jj], col(cf, (2, 9)[hv - 1]), ALU.is_equal, [vid0, "cf"], ["MJ%d" % hv], jj)
 
-    iota(T.W[:, 0:V], [[0, V]], OFF, [("W", 0, V)], V)
-    dma([(T.W[:, V * c:V * c + V], T.W[:, 0:V]) for c in range(1, 8)] +
-        [(T.W[:, V * c + V0:V * c + V], T.W[:, 0:V - V0]) for c in range(8, 16)], [("W", 0, V), "yBodd"],
-        [("W", V, 8 * V)] + [("W", V * c + V0, V * c + V) for c in range(8, 16)], 11.0)
-    dma([(T.W[S1, V * k:V * k + V0], T.yB[2 * k::16, 0:V0]) for k in range(8)], ["yB"], [("W", 0, 8 * V)], 1.5)
-    dma([(T.yA[:, 0:V0], T.y0[:])], [], [("yA", 0, V0)], 1.5, "G")
+    iota(T.W[:, WO:V], [[0, V0]], NONE, [("W", WO, V)], V0)
+    nxs, pvs = [slot(k, 0) for k in range(1, 8)], [slot(k, 1) for k in range(8)]
+    dma([(T.W[:, V * c:V * c + V], T.W[:, 0:V]) for c in nxs] + [(T.W[:, V * c:V * c + WO], T.W[:, 0:WO]) for c in pvs], [("W", 0, V), "NB0b"],
+        [("W", V * c, V * c + V) for c in nxs] + [("W", V * c, V * c + WO) for c in pvs], 11.0)
+    dma([(T.W[S1, V * slot(k, 0) + WO:V * slot(k, 0) + V], T.NB0[2 * k::16, OLD:U]) for k in range(8)], ["NB0"],
+        [("W", V * slot(k, 0), V * slot(k, 0) + V) for k in range(8)], 1.5)
+    dma([(T.yA[:, OLD:U], T.y0[:])], [], [("yA", OLD, U)], 1.5, "G")
+
+    def nb_of(t):
+        nm = "NB%d" % (t % 2)
+        return T[nm], [nm, nm + "b"]
 
     def search_steps(t, s):
-        have = V0 + M * t
-        xv, xn = (T.xc[:, have:have + M], "xc") if s == 0 else (T.xr[:, M * t:M * t + M], "xr")
+        new = first_new(t)
+        xv, xn = (T.xc[:, new:new + M], "xc") if s == 0 else (T.xr[:, M * t:M * t + M], "xr")
         st, sn = (T.st16, "st16") if s == 0 else (T.str16, "str16")
         st = st[:, 8 * t:8 * t + 8]
-        n = dict((k, k + str(s)) for k in ("pl", "c16", "cF", "hr", "xT", "sc", "best", "low", "lowb", "sd", "ia", "im", "iF", "ih", "a", "m", "K"))
+        n = dict((k, k + str(s)) for k in ("pl", "c16", "cF", "hr", "sc", "best", "low", "lowb", "sd", "ia", "im", "iF", "ih", "d", "r", "ve", "K"))
         b = dict((k, T[v]) for k, v in n.items())
-        xw, K = T.xc[:, 0:have], b["K"]
+        xw, K = T.xc[:], b["K"]
+        nb, nbn = nb_of(t)
+        nv, nm = ON_VECTOR[t][s], MIXED[t][s]
 
         def begin():
-            mm([(K[:, 0:128], xv, T.Ib[:], 128, False)], [xn, "Ib"], [n["K"]])
-            act(b["xT"][:], K[:, 0:128], [n["K"]], [n["xT"]], 128)
-            act(b["ia"][:], xw.indirect(st), ["xc", sn], [n["ia"]], 128, GA)
-            act(b["iF"][:], T.VID[:].indirect(st), ["VID", sn], [n["iF"]], 128, GA, ACT.Identity, bias=4112.0)
-            act(b["ih"][:], T.VID[:].indirect(st), ["VID", sn], [n["ih"]], 128, GA, ACT.Identity, bias=4096.0)
-            tt(b["im"][:], xw.indirect(st), xv, ALU.max, ["xc", xn, sn], [n["im"]], 128, GA)
+            ve = b["ve"]
+            for c in (0, 8):
+                sel(ve[:, c:2048:16], xv, [[0, M]], ALU.is_equal, 0.0, 0, 0, [xn], [n["ve"]], M)
+            for c in (8, 4, 2):
+                sel(ve[:, c // 2:2048:c], ve[:, 0:2048:c], [[0, 2048 // c]], ALU.is_equal, 0.0, 0, 0, [n["ve"]], [n["ve"]], 2048 // c)
+            tt(b["ia"][:], T.xc[:, OLD:U].indirect(st), ve[:, 0:2048:16], ALU.subtract, ["xc", n["ve"], sn], [n["ia"]], 128, GA)
+            ts(b["im"][:], b["ia"][:], 0.0, ALU.max, [n["ia"]], [n["im"]], 128, 0.5)
+            act(b["iF"][:], T.VID[:, OLD:U].indirect(st), ["VID", sn], [n["iF"]], 128, GA, ACT.Identity, bias=4112.0)
+            act(b["ih"][:], T.VID[:, OLD:U].indirect(st), ["VID", sn], [n["ih"]], 128, GA, ACT.Identity, bias=4096.0)
             mm([(K[:, 0:16], b["ih"][:], T.HR[:, 0:256:16], 16, False), (K[:, 0:8], b["iF"][:], T.If[:, 0:128:16], 8, True),
-                (K[:, 8:16], T.ones[:, 0:128], T.NEG[:], 8, False), (K[:, 0:16], xv, T.BOX[:, 0:256:16], 16, False),
-                (K[:, 0:16], b["ia"][:], T.BOX[:, 0:256:16], 16, False), (K[:, 0:16], b["im"][:], T.BO2[:], 16, False)],
-               [n["ih"], n["iF"], n["ia"], n["im"], xn, "HR", "If", "ones", "NEG", "BOX", "BO2"], [n["K"]])
+                (K[:, 8:16], T.ones[:, 0:128], T.NEG[:], 8, False),
+                (K[:, 0:16], b["ia"][:], T.BOX[:], 16, False), (K[:, 0:16], b["im"][:], T.BO2[:], 16, False)],
+               [n["ih"], n["iF"], n["ia"], n["im"], "HR", "If", "ones", "NEG", "BOX", "BO2"], [n["K"]])
             copy(b["best"][:], K[:, 0:16], [n["K"]], [n["best"]], 16)
 
         def step(h):
-            pl, pn = (st, sn) if h == 0 else (b["pl"][:], n["pl"])
-            nb = T.NBf[:, 0:have]
-            copy(b["c16"][:], T.NBi[:, 0:have].indirect(pl), [("NBi", 0, have), pn], [n["c16"]], 128, GA)
-            for q in range(4):
-                lo, vr = 512 * q, "VR%d%d" % (s, q % 2)
-                act(b["a"][:, lo:lo + 512], xw.indirect(b["c16"][:, 32 * q:32 * q + 32]), ["xc", n["c16"]], [(n["a"], lo, lo + 512)], 512, GA)
-                mm([(T[vr][:], b["xT"][:], T.EXP[:, lo:lo + 512], 512, False)], [n["xT"], "EXP"], [vr])
-                tt(b["m"][:, lo:lo + 512], b["a"][:, lo:lo + 512], T[vr][:], ALU.max, [(n["a"], lo, lo + 512), vr], [(n["m"], lo, lo + 512)], 512, 1.0)
-            act(b["hr"][:], nb.indirect(pl), ["NBf", pn], [n["hr"]], 128, GA, ACT.Identity, bias=4096.0)
-            act(b["cF"][:], nb.indirect(pl), ["NBf", pn, "cf"], [n["cF"]], 128, GA, ACT.Identity, bias=col(cf, 17 + h))
+            at, rd = (nb[:, OLD:U].indirect(st), [(x, OLD, U) for x in nbn] + [sn]) if h == 0 else (nb[:].indirect(b["pl"][:]), nbn + [n["pl"]])
+            ts(b["c16"][:], at, 0.25, ALU.add, rd, [n["c16"]], 128, GA)
+            act(b["hr"][:], at, rd, [n["hr"]], 128, GA, ACT.Identity, bias=4096.0)
+            act(b["cF"][:], at, rd + ["cf"], [n["cF"]], 128, GA, ACT.Identity, bias=col(cf, 17 + h))
             mm([(K[:, 0:256], b["hr"][:], T.HR[:], 256, False), (K[:, 0:128], b["cF"][:], T.If[:], 128, True),
-                (K[:, 128:256], T.ones[:, 0:128], T.PR[:, 128 * h:128 * h + 128], 128, False), (K[:, 0:256], xv, T.BOX[:], 256, False)],
-               [n["hr"], n["cF"], xn, "HR", "If", "ones", "PR", "BOX"], [n["K"]], True, False)
-            mm([(K[:, c:256:16], b["a"][:, c:2048:16], T.BOX[:, 0:256:16], 16, False) for c in range(16)], [n["a"], "BOX"], [n["K"]], False, False)
-            mm([(K[:, c:256:16], b["m"][:, c:2048:16], T.BO2[:], 16, False) for c in range(16)], [n["m"], "BO2"], [n["K"]], False, True)
+                (K[:, 128:256], T.ones[:, 0:128], T.PR[:, 128 * h:128 * h + 128], 128, False)],
+               [n["hr"], n["cF"], "HR", "If", "ones", "PR"], [n["K"]], True, False)
+            for (lo, hi, mixed) in ((512 * nv, 512 * (nv + nm), True), (0, 512 * nv, False)):
+                if lo == hi:
+                    continue
+                td, tr = (n["d"], lo, hi), (n["r"], lo, hi)
+                tt(b["d"][:, lo:hi], xw.indirect(b["c16"][:, lo // 16:hi // 16]), b["ve"][:, lo:hi], ALU.subtract, ["xc", n["c16"], n["ve"]], [td], hi - lo, GA)
+                if mixed:
+                    act(b["r"][:, lo:hi], b["d"][:, lo:hi], [td], [tr], hi - lo, 1.0, ACT.Abs, scale=0.5)
+                else:
+                    ts(b["r"][:, lo:hi], b["d"][:, lo:hi], 0.0, ALU.max, [td], [tr], hi - lo, 0.5)
+                    mm([(K[0:32 * nv, c:256:16], b["d"][:, c:hi:16], T.BOX[:], 16, False) for c in range(16)], [td, "BOX"], [n["K"]], False, False)
+            for q in range(nv + nm, 4):
+                lo, vr = 512 * q, "VR%d%d" % (s, q % 2)
+                td, tr = (n["d"], lo, lo + 512), (n["r"], lo, lo + 512)
+                act(b["d"][:, lo:lo + 512], xw.indirect(b["c16"][:, 32 * q:32 * q + 32]), ["xc", n["c16"]], [td], 512, GA)
+                mm([(T[vr][:], T.Ib[:], b["d"][:, lo:lo + 512], 512, False), (T[vr][:], minus, b["ve"][:, lo:lo + 512], 512, False)],
+                   [td, n["ve"], "Ib", "HR"], [vr])
+                act(b["r"][:, lo:lo + 512], T[vr][:], [vr], [tr], 512, 1.0, ACT.Abs, scale=0.5)
+            mm([(K[:, c:256:16], b["r"][:, c:2048:16], T.BO2[:], 16, False) for c in range(16)], [n["r"], "BO2"], [n["K"]], False, True)
             scan(b["sc"][:], T.RST[:], K[:, 0:256], ["RST", n["K"]], [n["sc"]], 256)
             tt(b["best"][:], b["sc"][:, 15:256:16], b["best"][:], ALU.min, [n["sc"], n["best"]], [n["best"]], 16)
             ts(b["low"][:], b["best"][:], 63, ALU.bitwise_and, [n["best"]], [n["low"]], 16)
@@ -352,41 +480,55 @@ def build_ops(g, core, T, topo):
                [(K[:, 8 * u:8 * u + 8], T.SELU[:, 128 * u:128 * u + 128], b["lowb"][:, 8 * w:8 * w + 8], 8, False) for u in range(8) for w in range(2)],
                ["Ib", "C2", "SELU", n["lowb"]], [n["K"]])
             scan(b["sd"][:], T.RST[:, 0:128:2], K[:, 0:64], ["RST", n["K"]], [n["sd"]], 64)
-            copy(b["pl"][:], b["sd"][:, 7:64:8], [n["sd"]], [n["pl"]], 8)
+            ts(b["pl"][:], b["sd"][:, 7:64:8], -float(new + M) if s == 1 and h == HOPS - 1 else 0.0, ALU.add, [n["sd"]], [n["pl"]], 8)
 
         return begin, step
 
     def send_y(t):
-        have = V0 + M * t
+        new = first_new(t)
         src = T.ysend[:, M * t:M * t + M]
-        act(src, T.yA[:, 0:have].indirect(T.pl1[:]), [("yA", 0, have), "pl1"], [("ysend", M * t, M * t + M)], 128, GA)
+        if EARLY[t]:
+            nb, nbn = nb_of(t)
+            yw, ty = T.yB[:, new + M:U], ("yB", new + M, U)
+            ts(T.c161[:], nb[:, new + M:U].indirect(T.pl1[:]), 0.25 - new - M, ALU.add, nbn + ["pl1"], ["c161"], 128, GA)
+            act(T.cF1[:], yw.indirect(T.pl1[:]), [ty, "pl1"], ["cF1"], 128, GA)
+            mm([(T.K1[:, 0:128], T.Ih[:], T.cF1[:], 128, True)], ["Ih", "cF1"], ["K1"], True, False)
+            for x in range(2):
+                at, tp = ring(1024)
+                act(T.PS[:, at:at + 1024], yw.indirect(T.c161[:, 64 * x:64 * x + 64]), [ty, "c161"], [tp], 1024, GA)
+                tt(T.PS[:, at:at + 1024:2], T.PS[:, at:at + 1024:2], T.PS[:, at + 1:at + 1024:2], ALU.mult, [tp], [tp], 512)
+                mm([(T.K1[:, 64 * x:64 * x + 64], T.In[:], T.PS[:, at + 2 * k:at + 1024:16], 64, True) for k in range(8)], [tp, "In"], ["K1"], False, x == 1)
+            shift(src, T.K1[:, 0:128], 0.5, ["K1"], [("ysend", M * t, M * t + M)], 128)
+        else:
+            act(src, T.yA[:, new + M:U].indirect(T.pl1[:]), [("yA", new + M, U), "pl1"], [("ysend", M * t, M * t + M)], 128, GA)
         rid, pid = topo.addr(near(t), core)
         engs = widest(topo.engines(core, near(t)))
         sem = T.sem["ry%d" % t]
         sent[0] += len(engs)
-        s = add("G", lambda: [g.remote_dma(T.yA[:, have:have + M], src, sem, T.sem.sent, pid, rid, mask_of(engs))],
-                [("ysend", M * t, M * t + M)], [], 1.0, 3.0, "remote")
-        add("none", None, [], [("yA", have, have + M)], 0.0, 0.0, "recv", [s], ("ry%d" % t, len(widest(topo.engines(far(t), core)))))
+        s = add("G", lambda: [g.remote_dma(T.yA[:, new:new + M], src, sem, T.sem.sent, pid, rid, mask_of(engs))],
+                [("ysend", M * t, M * t + M)], [], 1.0, 3.5, "remote")
+        add("none", None, [], [("yA", new, new + M)], 0.0, 0.0, "recv", [s], ("ry%d" % t, len(widest(topo.engines(far(t), core)))))
 
     def enter(t):
-        have = V0 + M * t
-        now = have + M
-        pl, nb, xw = T.pl0[:], T.NBf[:, 0:have], T.xc[:, 0:have]
-        hk = [(h, k) for h in range(2) for k in range(8)]
-        K, R = T.K0, T.VR00
-        enc = OFF - ENC * (t + 1)
-        iota(T.WENC[:], [[1, 128], [0, 8]], have + enc, ["WENC"], 1024)
-        shift(T.WL[:], T.VID[:, have:now:2], col(cf, 5), ["VID", "cf"], ["WL"], 64)
-        shift(T.WLe[:], T.WL[:], float(enc), ["WL"], ["WLe"], 64)
-        shift(T.BASE[:, 0:64], T.WL[:], col(cf, 12), ["WL", "cf"], [("BASE", 0, 64)], 64)
-        shift(T.BASE[:, 64:128], T.WL[:], col(cf, 13), ["WL", "cf"], [("BASE", 64, 128)], 64)
-        copy(T.cb[:], nb.indirect(pl), ["NBf", "pl0"], ["cb"], 128, GA)
-        mm([(R[:, 0:64], zmat(2 * ((k + 1) % 8), 8 * h + k), T.cb[:, h:128:2], 64, False) for (h, k) in hk], ["Z", "cb"], ["VR00"])
-        copy(T.CL16[:], R[:, 0:64], ["VR00"], ["CL16"], 64)
-        tt(T.P1[:, 0:64], R[:, 0:64], T.WL[:], ALU.subtract, ["VR00", "WL"], [("P1", 0, 64)], 64, 1.0)
-        copy(T.G1[:], nb.indirect(T.CL16[:]), ["NBf", "CL16"], ["G1"], 1024, GA)
+        new = first_new(t)
+        now = U - new
+        nb, nbn = nb_of(t)
+        pl, xw = T.pl0[:], T.xc[:]
+        nn = "NB%d" % ((t + 1) % 2)
+        HV = HALVES[t]
+        KK, JJ = 8 // HV, 2 * HV
+        UW, GW, n = M // JJ, 8 * KK, 1024 // HV
+        jk = [(jj, kk) for jj in range(JJ) for kk in range(KK)]
+        cj, LX, lx, UU, uu, MJ, mj = 20 + 3 * (HV - 1), T["LX%d" % HV], "LX%d" % HV, T["UU%d" % HV], "UU%d" % HV, T["MJ%d" % HV], "MJ%d" % HV
+        iota(T.WENC[:, 0:n], [[1, 128], [0, KK]], new, ["WENC"], n)
+        for e in range(HV):
+            shift(T.WL[:, UW * e:UW * e + UW], T.VID[:, new:new + M:JJ], col(cf, cj), ["VID", "cf"], [("WL", UW * e, UW * e + UW)], UW)
+        wl, twl = T.WL[:, 0:UW], ("WL", 0, UW)
+        for d in range(2):
+            shift(T.BASE[:, UW * d:UW * d + UW], wl, col(cf, cj + 1 + d), [twl, "cf"], [("BASE", UW * d, UW * d + UW)], UW)
+        copy(T.cb[:], nb[:].indirect(pl), nbn + ["pl0"], ["cb"], 128, GA)
         copy(T.brep[:], T.VID[:].indirect(pl), ["VID", "pl0"], ["brep"], 128, GA)
-        ts(T.nbrep[:], T.VID[:].indirect(pl), -1.0, ALU.mult, ["VID", "pl0"], ["nbrep"], 128, GA)
+        ts(T.nbrep[:], T.brep[:], -1.0, ALU.mult, ["brep"], ["nbrep"], 128, 0.5)
         for x in range(2):
             vr = "VR0%d" % x
             lst = [(T[vr][:], T.nbrep[:], T.SEL[:, 512 * x:512 * x + 512], 512, False)]
@@ -395,143 +537,216 @@ def build_ops(g, core, T, topo):
                 lst += [(o, T.SEL[:, 512 * x + 128 * q:512 * x + 128 * q + 128], T.brep[:], 128, False), (o, T.Ib[:], T.TRI[:], 128, False)]
             mm(lst, ["nbrep", "brep", "SEL", "Ib", "TRI"], [vr])
             ts(T.E[:, 512 * x:512 * x + 512], T[vr][:], 0.0, ALU.is_equal, [vr], [("E", 512 * x, 512 * x + 512)], 512)
-        for d in range(2):
-            mm([(K[:, 64 * d:64 * d + 64], zmat(2 * k + d, 8 * h + k), T.G1[:, 8 * h + k:1024:16], 64, False) for (h, k) in hk], ["Z", "G1"], ["K0"])
-        copy(T.FA16[:], K[:, 0:128], ["K0"], ["FA16"], 128)
-        tt(T.P1[:, 64:128], K[:, 0:64], T.WL[:], ALU.subtract, ["K0", "WL"], [("P1", 64, 128)], 64, 1.0)
-        tt(T.P2[:, 192:256], K[:, 64:128], T.WL[:], ALU.subtract, ["K0", "WL"], [("P2", 192, 256)], 64, 1.0)
-        shift(T.P1[:, 128:192], T.P1[:, 0:64], float(8 * V), [("P1", 0, 64)], [("P1", 128, 192)], 64)
-        shift(T.P1[:, 192:256], T.P2[:, 192:256], -float(8 * V), [("P2", 192, 256)], [("P1", 192, 256)], 64)
-        act(T.P2[:, 0:64], T.P1[:, 64:128], [("P1", 64, 128)], [("P2", 0, 64)], 64)
-        act(T.P2[:, 64:128], T.P1[:, 0:64], [("P1", 0, 64)], [("P2", 64, 128)], 64)
-        act(T.P2[:, 128:192], T.P1[:, 0:64], [("P1", 0, 64)], [("P2", 128, 192)], 64)
-        for d in range(2):
-            lo = 1024 * d
-            act(T.a0[:, lo:lo + 1024], xw.indirect(T.FA16[:, 64 * d:64 * d + 64]), ["xc", "FA16"], [("a0", lo, lo + 1024)], 1024, GA)
-            tt(T.m0[:, lo:lo + 1024], xw.indirect(T.CL16[:]), T.a0[:, lo:lo + 1024], ALU.max, ["xc", "CL16", ("a0", lo, lo + 1024)], [("m0", lo, lo + 1024)], 1024, GA)
-        for q in range(2):
-            vr = "VR0%d" % q
-            mm([(T[vr][:], T.xT0[:], T.EXP[:, 1024 * q:1024 * q + 1024:2], 512, False)], ["xT0", "EXP"], [vr])
-        for d in range(2):
-            for q in range(2):
-                lo, vr = 1024 * d + 512 * q, "VR0%d" % q
-                tt(T.mv[:, lo:lo + 512], T.a0[:, lo:lo + 512], T[vr][:], ALU.max, [("a0", lo, lo + 512), vr], [("mv", lo, lo + 512)], 512, 1.0)
-        neg = T.BOX[:, 0:128:16]
-        for k in range(8):
-            o = K[:, k:64:8]
-            mm([(o, T.m0[:, k:1024:8], T.BOP[:], 8, False), (o, T.mv[:, k:1024:8], neg, 8, False),
-                (o, T.m0[:, 1024 + k:2048:8], neg, 8, False), (o, T.mv[:, 1024 + k:2048:8], T.BOP[:], 8, False)],
-               ["m0", "mv", "BOX", "BOP"], ["K0"])
-        ts(T.CH[:, 0:64], K[:, 0:64], 0.0, ALU.is_ge, ["K0"], [("CH", 0, 64)], 64)
-        ts(T.CH[:, 64:128], K[:, 0:64], 0.0, ALU.is_lt, ["K0"], [("CH", 64, 128)], 64)
-        for w in range(2):
-            mm([(R[:, 64 * w:64 * w + 64], T.Ib[:], T.CH[:, 64 - 64 * w:128 - 64 * w], 64, False)] +
-               [(R[:, 64 * w + 8 * q:64 * w + 8 * q + 8], T.E[:, 128 * q:128 * q + 128], T.CH[:, 64 * w + 8 * q:64 * w + 8 * q + 8], 8, False)
-                for q in range(8)], ["Ib", "CH", "E"], ["VR00"])
-        for h in range(2):
-            ts(T.LX[:, :, h, :], R[:, 0:128], 0.0, ALU.is_equal, ["VR00", "cf"], [("LX", h, h + 1)], 128, 1.0, col(cf, 10 if h == 0 else 2), ALU.mult)
-        for q in range(4):
-            mm([(K[:, 64 * q:64 * q + 64], T.LX[:, 8 * (q // 2):8 * (q // 2) + 8, :, :], T.U[:], 64, False)], ["LX", "U"], ["K0"])
-        tt(T.t1[:], K[:, 0:256], T.P1[:], ALU.mult, ["K0", "P1"], ["t1"], 256, 1.0)
-        tt(T.s1[:], T.t1[:, 0:128], T.t1[:, 128:256], ALU.add, ["t1"], ["s1"], 128)
-        tt(T.s2[:], T.s1[:], T.BASE[:], ALU.add, ["s1", "BASE"], ["s2"], 128)
-        copy(T.O16[:], T.s2[:], ["s2"], ["O16"], 128)
-        tt(T.t2[:], K[:, 0:256], T.P2[:], ALU.mult, ["K0", "P2"], ["t2"], 256, 1.0)
-        tt(T.HT[:], T.t2[:, 0:128], T.t2[:, 128:256], ALU.add, ["t2"], ["HT"], 128)
-        act(T.W[:].indirect(T.O16[:, 0:64]), T.WENC[:], ["O16", "WENC"], ["W"], 1024, SCA, ACT.Silu)
-        tt(T.IV[:], T.W[:].indirect(T.O16[:, 64:128]), T.WENC[:], ALU.min, ["W", "O16", "WENC"], ["IV"], 1024, GA)
-        act(T.W[:].indirect(T.O16[:, 64:128]), T.IV[:], ["O16", "IV"], ["W"], 1024, SCA, ACT.Silu)
-        dma([(T.NBraw[0::2, :], T.W[S1, 0:8 * V]), (T.NBraw[1::2, :], T.W[S2, 8 * V:16 * V])], ["W"], ["NBraw"], 1.5)
+        neg = T.BOX[:, 0:8]
+
+        def half(e):
+            kn, rn = (("K0", "VR00"), ("SW0", "SW1"))[e]
+            K, R = T[kn], T[rn]
+
+            def piece(nm, per, a, z):
+                lo, hi = UW * (per * e + a), UW * (per * e + z)
+                return T[nm][:, lo:hi], (nm, lo, hi)
+
+            mm([(R[:, 0:UW], zmat(2 * ((HV * kk + e + 1) % 8), KK * jj + kk), T.cb[:, jj:128:JJ], UW, False) for (jj, kk) in jk], ["Z", "cb"], [rn])
+            (cl, tcl), (fa, tfa), pp = piece("CL16", 1, 0, 1), piece("FA16", 2, 0, 2), [piece("P1", 4, x, x + 1) for x in range(4)]
+            copy(cl, R[:, 0:UW], [rn], [tcl], UW)
+            tt(pp[0][0], R[:, 0:UW], wl, ALU.subtract, [rn, twl], [pp[0][1]], UW, 1.0)
+            act(pp[2][0], pp[0][0], [pp[0][1]], [pp[2][1]], UW)
+            tg = ("G1", n * e, n * e + n)
+            copy(T.G1[:, n * e:n * e + n], nb[:].indirect(cl), nbn + [tcl], [tg], n, GA)
+            for d in range(2):
+                mm([(K[:, UW * d:UW * d + UW], zmat(2 * (HV * kk + e) + d, KK * jj + kk), T.G1[:, n * e + KK * jj + kk:n * e + n:16], UW, False)
+                    for (jj, kk) in jk], ["Z", tg], [kn])
+            copy(fa, K[:, 0:2 * UW], [kn], [tfa], 2 * UW)
+            for d in range(2):
+                tt(pp[1 + 2 * d][0], K[:, UW * d:UW * d + UW], wl, ALU.subtract, [kn, twl], [pp[1 + 2 * d][1]], UW, 1.0)
+            mm([(K[:, 0:GW], T.Ib[:], T.ZERO[:, 0:GW], GW, False)], ["Ib", "ZERO"], [kn], True, False)
+            for d in range(2):
+                lo = n * (2 * e + d)
+                act(T.d0[:, lo:lo + n], xw.indirect(piece("FA16", 2, d, d + 1)[0]), ["xc", tfa], [("d0", lo, lo + n)], n, GA)
+                tt(T.r0[:, lo:lo + n], xw.indirect(cl), T.d0[:, lo:lo + n], ALU.max, ["xc", tcl, ("d0", lo, lo + n)], [("r0", lo, lo + n)], n, GA)
+                for q in range(n // 512):
+                    a, vr = lo + 512 * q, ("VR01", rn)[(d + q) % 2]
+                    mm([(T[vr][:], T.Ib[:], T.d0[:, a:a + 512], 512, False), (T[vr][:], minus, T.ve0[:, 512 * JJ * q:512 * JJ * (q + 1):JJ], 512, False)],
+                       [("d0", a, a + 512), "ve0", "Ib", "HR"], [vr])
+                    act(T.mv[:, a:a + 512], T[vr][:], [vr], [("mv", a, a + 512)], 512, 1.0, ACT.Relu)
+                for (nm, sign) in (("r0", (T.BOP[:], neg)[d]), ("mv", (neg, T.BOP[:])[d])):
+                    mm([(K[:, kk:GW:KK], T[nm][:, lo + kk:lo + n:KK], sign, 8, False) for kk in range(KK)], [(nm, lo, lo + n), "BOX", "BOP"], [kn],
+                       False, nm == "mv" and d == 1)
+            ch, tch = 2 * GW * e, ("CH", 2 * GW * e, 2 * GW * e + 2 * GW)
+            ts(T.CH[:, ch:ch + GW], K[:, 0:GW], 0.0, ALU.is_ge, [kn], [("CH", ch, ch + GW)], GW)
+            ts(T.CH[:, ch + GW:ch + 2 * GW], K[:, 0:GW], 0.0, ALU.is_lt, [kn], [("CH", ch + GW, ch + 2 * GW)], GW)
+            mm([(K[:, 4 * UW:6 * UW], T.If[:], T.BASE[:, 0:2 * UW], 2 * UW, True)], ["If", "BASE"], [kn], True, False)
+            for w in range(2):
+                own, other = ch + GW * w, ch + GW * (1 - w)
+                mm([(R[:, GW * w:GW * w + GW], T.Ib[:], T.CH[:, other:other + GW], GW, False)] +
+                   [(R[:, GW * w + KK * q:GW * w + KK * q + KK], T.E[:, 128 * q:128 * q + 128], T.CH[:, own + KK * q:own + KK * q + KK], KK, False)
+                    for q in range(8)], ["Ib", tch, "E"], [rn])
+            for jj in range(JJ):
+                ts(LX[:, 16 * e:16 * e + 16, jj, :], R[:, 0:2 * GW], 0.0, ALU.is_equal, [rn, mj], [(lx, JJ * e + jj, JJ * e + jj + 1)], 2 * GW,
+                   1.0, col(MJ, jj), ALU.mult)
+            ahead, back, tlx = LX[:, 16 * e:16 * e + 8, :, :], LX[:, 16 * e + 8:16 * e + 16, :, :], (lx, JJ * e, JJ * e + JJ)
+            mm([(K[:, 4 * UW:6 * UW], back, UU[:, 2 * UW:4 * UW], 2 * UW, False)], [tlx, uu], [kn], False, True)
+            mm([(K[:, 0:2 * UW], ahead, UU[:, 0:2 * UW], 2 * UW, False)], [tlx, uu], [kn])
+            mm([(K[:, 2 * UW:4 * UW], back, UU[:, 0:2 * UW], 2 * UW, False)], [tlx, uu], [kn])
+            (t1, tt1), (s1, ts1), (s2, ts2), (o16, to) = piece("t1", 4, 0, 4), piece("s1", 2, 0, 2), piece("s2", 2, 0, 2), piece("O16", 2, 0, 2)
+            tt(t1, K[:, 0:4 * UW], piece("P1", 4, 0, 4)[0], ALU.mult, [kn, piece("P1", 4, 0, 4)[1]], [tt1], 4 * UW, 1.0)
+            tt(s1, piece("t1", 4, 0, 2)[0], piece("t1", 4, 2, 4)[0], ALU.add, [tt1], [ts1], 2 * UW)
+            tt(s2, s1, K[:, 4 * UW:6 * UW], ALU.add, [ts1, kn], [ts2], 2 * UW, 1.0)
+            copy(o16, s2, [ts2], [to], 2 * UW)
+            for d, (x, y) in enumerate(((1, 2), (0, 3))):
+                lo = 64 * d + UW * e
+                tt(T.HT[:, lo:lo + UW], piece("t1", 4, x, x + 1)[0], piece("t1", 4, y, y + 1)[0], ALU.add, [tt1], [("HT", lo, lo + UW)], UW)
+            wa, wz = 16 * V // HV * e, 16 * V // HV * (e + 1)
+            win, tw, iv, ti = T.W[:, wa:wz], ("W", wa, wz), T.IV[:, n * e:n * e + n], ("IV", n * e, n * e + n)
+            near_end, far_end = piece("O16", 2, 0, 1)[0], piece("O16", 2, 1, 2)[0]
+            scatter(win.indirect(near_end), T.WENC[:, 0:n], [to, "WENC"], [tw], n, SCATTERS[t][2 * e])
+            tt(iv, win.indirect(far_end), T.WENC[:, 0:n], ALU.min, [tw, to, "WENC"], [ti], n, GA)
+            scatter(win.indirect(far_end), iv, [to, ti], [tw], n, SCATTERS[t][2 * e + 1])
+            mine = range(2) if HV == 1 else [e]
+            dma([(T[nn][2 * x + d::4, PAD:U], T.W[(S1, S2)[d], V * (8 * x + 4 * d):V * (8 * x + 4 * d + 4)]) for x in mine for d in range(2)],
+                [tw], [(nn + ("", "b")[x], PAD, U) for x in mine], 1.3 / HV)
+
+        for e in range(HV):
+            half(e)
+        K, R = T.K0, T.VR00
         mm([(R[:, 0:64], T.Zf[:, 15 - c:143 - c], T.IV[:, c:1024:16], 64, True) for c in range(16)], ["Zf", "IV"], ["VR00"])
-        tt(T.win[:], R[:, 0:64], T.WLe[:], ALU.is_equal, ["VR00", "WLe"], ["win"], 64, 1.0)
+        tt(T.win[:], R[:, 0:64], T.WL[:], ALU.is_equal, ["VR00", "WL"], ["win"], 64, 1.0)
         for d in range(2):
             lo = 64 * d
             tt(T.nw[:, lo:lo + 64], T.win[:], T.HT[:, lo:lo + 64], ALU.mult, ["win", "HT"], [("nw", lo, lo + 64)], 64)
             tt(T.NEW[:, lo:lo + 64], T.nw[:, lo:lo + 64], T.WL[:], ALU.add, [("nw", lo, lo + 64), "WL"], [("NEW", lo, lo + 64)], 64)
-        for h in range(2):
-            mm([(K[:, h:128:2], zmat(8 * h + k, 2 * k + d), T.NEW[:, 64 * d:64 * d + 64], 64, False) for k in range(8) for d in range(2)],
-               ["Z", "NEW"], ["K0"])
-        copy(T.NBi[:, have:now], K[:, 0:128], ["K0"], [("NBi", have, now)], 128)
-        if t + 1 < RO:
-            shift(T.NWB[:], K[:, 0:128], float(OFF), ["K0"], ["NWB"], 128)
-        copy(T.NBi[:, 0:have], T.NBraw[:, 0:have], ["NBraw"], [("NBi", 0, have)], have)
-        ts(T.NBi[:, 0:have], T.NBi[:, 0:have], ENC - 1, ALU.bitwise_and, [("NBi", 0, have)], [("NBi", 0, have)], have)
-        copy(T.NB16[:, 0:now], T.NBi[:, 0:now], ["NBi"], ["NB16"], now)
-        copy(T.NBf[:, 0:now], T.NBi[:, 0:now], ["NBi"], ["NBf"], now)
-        al, bl = "AL%d" % (t % 2), "BL%d" % (t % 2)
-        dma([(T[al][:, 0:now // 2], T.NB16[0::2, 0:now]), (T[bl][:, 0:now // 2], T.NB16[1::2, 0:now])], ["NB16"], [al, bl], 0.6)
-        if t + 1 < RO:
-            dma([(T.W[S1, V * k + have:V * k + now], T.NWB[2 * k::16, :]) for k in range(8)] +
-                [(T.W[S2, V * (8 + k) + have:V * (8 + k) + now], T.NWB[2 * k + 1::16, :]) for k in range(8)], ["NWB"], ["W"], 0.5)
-        else:
-            dma([(T.nx[:], T.NBf[0::2, :])], ["NBf"], [], 1.0)
+        for jj in range(JJ):
+            mm([(K[:, jj:128:JJ], zmat(KK * jj + kk, 2 * (HV * kk + e) + d), T.NEW[:, 64 * d + UW * e:64 * d + UW * e + UW], UW, False)
+                for kk in range(KK) for e in range(HV) for d in range(2)], ["Z", "NEW"], ["K0"])
+        act(T[nn][:, new:new + M], K[:, 0:128], ["K0"], [(nn, new, new + M), (nn + "b", new, new + M)], 128)
+        if t:
+            both = [(nn, new + M, OLD), (nn + "b", new + M, OLD)]
+            tt(T[nn][:, new + M:OLD], T[nn][:, new + M:OLD], nb[:, new + M:OLD], ALU.min, both + nbn, both, M * t)
+        Q, ls = now // 4, "LS%d" % (t % 2)
+        for q in range(4):
+            ts(T.NB16[:, Q * q:Q * q + Q], T[nn][:, new + q:U:4], 0.25 - new, ALU.add, [nn, nn + "b"], [("NB16", Q * q, Q * q + Q)], Q)
+        for d in range(2):
+            dma([(T[ls][kk::4, QM * (2 * d + e):QM * (2 * d + e) + Q], T.NB16[4 * kk + 2 * e + d::16, 0:now]) for e in range(2) for kk in range(4)],
+                ["NB16"], [(ls, 2 * QM * d, 2 * QM * d + 2 * QM)], 0.3)
+        if t + 1 == RO:
+            put_nx(T[nn], nn)
+
+    def put_nx(nb, nn):
+        H = V // 2
+        dma([(T.IV[0::2, 0:H], nb[0::2, OLD:OLD + H]), (T.IV[1::2, 0:V0 - H], nb[0::2, OLD + H:U])] +
+            [(T.IV[1::2, V0 - H + M * t:V0 - H + M * t + M], nb[0::2, first_new(t):first_new(t) + M]) for t in range(RO)], [nn, nn + "b"], ["IV"], 0.5)
+        num = T.Z[:, 0:H]
+        copy(num, T.IV[:, 0:H], ["IV"], ["Z"], H)
+        parts = [(T.d0[:, 0:H], ("d0", 0, H), first_new(1), 2 * M), (T.d0[:, H:V], ("d0", H, V), first_new(0), 2 * M), (T.r0[:, 0:H], "r0", OLD, V0 + M)]
+        for (o, nm, edge, drop) in parts:
+            ts(o, num, float(edge), ALU.is_ge, ["Z"], [nm], H, 0.5, -float(drop), ALU.mult)
+        for x in range(2):
+            lo, vr = QM * x, "VR0%d" % x
+            o = T[vr][:, 0:QM]
+            mm([(o, T.I16[:], T.Z[:, lo:lo + QM], QM, False), (o, T.Ib[:], T.d0[:, lo:lo + QM], QM, False),
+                (o, T.Ib[:], T.d0[:, H + lo:H + lo + QM], QM, False), (o, T.Ib[:], T.r0[:, lo:lo + QM], QM, False)], ["I16", "Ib", "Z", "d0", "r0"], [vr])
+            shift(T.WENC[:, lo:lo + QM], o, float(V - M - PAD), [vr], [("WENC", lo, lo + QM)], QM)
+        dma([(T.nx[:], T.WENC[:, 0:H])], ["WENC"], [], 0.7)
+
+    def put_y(lo, hi):
+        pairs = []
+        while lo < hi:
+            if lo >= OLD:
+                end, to = hi, lo - OLD
+            else:
+                blk = (lo - PAD) // M
+                end, to = min(hi, PAD + M * blk + M), V0 + M * (RO - 1 - blk) + lo - PAD - M * blk
+            pairs.append((T.y[:, to:to + end - lo], T.yA[:, lo:end]))
+            lo = end
+        return pairs
 
     turn = [0, 0]
 
+    def ring(n):
+        if turn[1] + n > RING:
+            turn[1] = 0
+        turn[1] += n
+        return turn[1] - n, ("PS", turn[1] - n, turn[1])
+
     def sweeps(t):
-        now = V0 + M * (t + 1)
-        H = now // 2
-        al, bl = "AL%d" % (t % 2), "BL%d" % (t % 2)
-        nch, n = H // CU, 16 * CU
-        groups = [list(range(a, min(a + 4, nch - 1))) for a in range(0, nch - 1, 4)] + [[nch - 1]]
-        alone = t == RO - 1
+        new = first_new(t)
+        ls = "LS%d" % (t % 2)
+        banks = SWEEP_BANKS[t]
+        if SCANS[t]:
+            sel(T.E[:], T.ones[:], [[0, 256], [1, 4]], ALU.is_gt, 0.0, 0, 0, ["ones"], ["E"], 1024)
         for s in range(SWEEPS):
             src, dst = ("yA", "yB") if s == 0 else ("yB", "yA")
-            yw = T[src][:, 0:now]
-            if alone and s == 0:
-                shift(T.NBraw[:], T.yA[:], 0.5, ["yA"], ["NBraw"], V, scale=0.5)
-            for grp in groups:
-                bank = "SW%d" % (turn[0] % 2)
+            yw, ty = T[src][:, new:U], (src, new, U)
+            u = 0
+            for c, wd in enumerate(CHUNKS[t]):
+                if s == SWEEPS - 1 and t + 1 < RO and EARLY[t + 1] == c + 1:
+                    send_y(t + 1)
+                n = 16 * wd
+                bank = banks[turn[0] % len(banks)]
                 turn[0] += 1
-                for q, j in enumerate(grp):
-                    ia, ip = n * (turn[1] % NBUF), n * (NBUF + turn[1] % NBUF)
-                    turn[1] += 1
-                    A, P = T.PS[:, ia:ia + n], T.PS[:, ip:ip + n]
-                    ta, tp = ("PS", ia, ia + n), ("PS", ip, ip + n)
-                    act(A, yw.indirect(T[al][:, CU * j:CU * j + CU]), [(src, 0, now), al], [ta], n, GA)
-                    tt(P, yw.indirect(T[bl][:, CU * j:CU * j + CU]), A, ALU.mult, [(src, 0, now), bl, ta], [tp], n, GA)
-                    for h in range(2):
-                        o = T[bank][:, 256 * h + CU * q:256 * h + CU * q + CU]
-                        mm(([] if alone else [(o, T.Ih[:], T[src][:, H * h + CU * j:H * h + CU * j + CU], CU, True)]) +
-                           [(o, T.In[:], T.PS[:, ip + 2 * k + h:ip + n:16], CU, True) for k in range(8)],
-                           [tp, (src, 0, now), "Ih", "In"], [bank])
-                wd, outs = CU * len(grp), []
-                for h in range(2):
-                    lo = H * h + CU * grp[0]
-                    o, ps, tk = T[dst][:, lo:lo + wd], T[bank][:, 256 * h:256 * h + wd], (dst, lo, lo + wd)
-                    if alone:
-                        tt(o, T.NBraw[:, lo:lo + wd], ps, ALU.add, [bank, ("NBraw", lo, lo + wd)], [tk], wd, 1.0)
-                        if s + 1 < SWEEPS:
-                            shift(T.NBraw[:, lo:lo + wd], o, 0.5, [tk], [("NBraw", lo, lo + wd)], wd, scale=0.5)
-                    else:
-                        shift(o, ps, 0.5, [bank], [tk], wd)
-                    outs.append(lo)
+                lo, hi = new + 4 * u, new + 4 * (u + wd)
+                o = T[bank][:, 0:4 * wd]
+                mm([(o, T.Ih[:], T[src][:, lo:hi], 4 * wd, True)], [(src, lo, hi), "Ih"], [bank], True, False)
+                for e in range(2):
+                    at, tp = ring(n)
+                    P = T.PS[:, at:at + n]
+                    la, lb = QM * e + u, QM * (2 + e) + u
+                    act(P, yw.indirect(T[ls][:, la:la + wd]), [ty, (ls, la, la + wd)], [tp], n, GA)
+                    tt(P, yw.indirect(T[ls][:, lb:lb + wd]), P, ALU.mult, [ty, (ls, lb, lb + wd), tp], [tp], n, GA)
+                    picks = range(4)
+                    if c in BY_DMA[t]:
+                        if e == 0:
+                            even = (at, tp, P)
+                            continue
+                        dma([(even[2], P)], [even[1], tp], [even[1]], n * 1.7e-3, "G", accum_op=ALU.add)
+                        at, tp = even[0], even[1]
+                    if (c, e) in SCANS[t]:
+                        at, tq = ring(n)
+                        vec(lambda o=T.PS[:, at:at + n], P=P, n=n: vq.tensor_tensor_scan(o, T.E[:, 0:n], P, 0.0, ALU.mult, ALU.add), [tp, "E"], [tq], n)
+                        tp, picks = tq, [3]
+                    mm([(o, T.In[:], T.PS[:, at + kk:at + n:4], 4 * wd, True) for kk in picks], [tp, "In"], [bank], False, e == 1)
+                if EVAC[t][c % len(EVAC[t])] == "V":
+                    ts(T[dst][:, lo:hi], o, 0.5, ALU.add, [bank], [(dst, lo, hi)], 4 * wd)
+                else:
+                    shift(T[dst][:, lo:hi], o, 0.5, [bank], [(dst, lo, hi)], 4 * wd)
                 if t == RO - 1 and s == SWEEPS - 1:
-                    dma([(T.y[:, lo:lo + wd], T[dst][:, lo:lo + wd]) for lo in outs], [(dst, lo, lo + wd) for lo in outs], [], 0.3)
+                    dma(put_y(lo, hi), [(dst, lo, hi)], [], 0.3)
+                u += wd
 
-    for t in range(RO):
-        parts = [search_steps(t, 0), search_steps(t, 1)]
-        for (begin, step) in parts:
+    def searches(t):
+        for s in range(2):
+            part[0] = ("own", "served")[s] + str(t)
+            begin, step = search_steps(t, s)
             begin()
-        for h in range(HOPS):
-            for (begin, step) in parts:
+            for h in range(HOPS):
                 step(h)
-        send_y(t)
+
+    searches(0)
+    send_y(0)
+    for t in range(RO):
+        part[0] = "enter" + str(t)
         enter(t)
+        if t + 1 < RO:
+            searches(t + 1)
+        part[0] = "sweeps" + str(t)
         sweeps(t)
+        if t + 1 < RO and not EARLY[t + 1]:
+            send_y(t + 1)
     return ops, sent[0]
 
 
 def rank_program(g, core, T, topo):
     if T.rank_of(core) is None:
         return
-    ops, sent = build_ops(g, core, T, topo)
-    order = plan_order(ops)
+    ops, sent = build_ops(g, core, T, topo, FIG)
+    if "order" not in PLAN:
+        PLAN["order"] = plan_order([build_ops(g, core, T, topo, f)[0] for f in FIGS])[1]
     queue = {"V": g.vector, "S": g.scalar, "P": g.tensor, "G": g, "Y": g.sync}
     count = {"V": 0, "S": 0, "P": 0, "G": 0}
     waited = dict((q, {}) for q in queue)
     final, ndma = {}, [0]
-    for i in order:
+    for i in PLAN["order"]:
         o = ops[i]
         if o["kind"] == "recv":
             o["done"] = o["sem"]

from concourse.bass import DstId, RemoteDMATransfer
from concourse.mybir import AluOpType as ALU, ActivationFunctionType as ACT

N, V0, M, RO, HOPS, SWEEPS = 4, 1024, 128, 3, 3, 2
V = V0 + RO * M
PAD = 32
U, OLD = PAD + V, PAD + RO * M
F32, BF, I32, U16, F16 = "float32", "bfloat16", "int32", "uint16", "float16"
ZW = 144
QM = V // 4
RING = 7168
BIG = 33554432.0
NONE = 2048
CHUNKS = [[48] * 6, [40] * 8, [24, 40, 48, 48, 48, 40, 48, 32, 24]]
SCANS = [[], [], [(7, 0), (7, 1), (8, 0), (8, 1)]]
SWEEP_BANKS = [["SW0", "SW1", "VR10"], ["SW0", "SW1", "VR10"], ["SW0", "SW1", "VR10", "VR11", "K1", "K0"]]
ON_VECTOR = [[2, 2], [2, 3], [2, 3]]
MIXED = [[0, 0], [0, 0], [0, 0]]
BY_DMA = [[0, 1, 2, 3, 4], [0, 1, 2, 3, 4, 5, 6], [0, 2, 4, 5]]
HALVES = [2, 1, 1]
SCATTERS = ["SVVS", "SS", "SS"]
EVAC = ["S", "S", "S"]
EARLY = [0, 0, 3]
INV_SPLIT = 14


def sb(w, d):
    return ("sbuf", [128] + (list(w) if isinstance(w, (list, tuple)) else [w]), d)


SCRATCH = {
    "W": sb(16 * V, F32), "PS": sb(RING, F32), "mv": sb(2048, BF), "yA": sb(U, F32), "yB": sb(U, F32),
    "NB0": sb(U, F32), "NB1": sb(U, F32), "NBi": sb(V0, I32), "NB16": sb(V, U16), "LS0": sb(4 * QM, U16), "LS1": sb(4 * QM, U16),
    "VID": sb(U, F32), "xc": sb(U, BF), "xr": sb(RO * M, BF),
    "sti": sb(24, I32), "st16": sb(24, U16), "str16": sb(24, U16),
    "Lraw": sb(512, I32), "L16": sb(512, U16), "IV": sb(V0, F32), "WENC": sb(V0, F32),
    "d0": sb(2048, BF), "d1": sb(2048, BF), "r0": sb(2048, BF), "r1": sb(2048, BF), "ve0": sb(2048, BF), "ve1": sb(2048, BF),
    "ones": sb(1024, BF), "SELU": sb(1024, BF), "SEL": sb(1024, F16),
    "Z": sb(16 * ZW, F16), "Zf": sb(ZW, F32), "RM": sb(16, F32),
    "Ib": sb(128, BF), "If": sb(128, F32), "Ih": sb(128, F32), "In": sb(128, F32), "I16": sb(128, F16),
    "HR": sb(256, BF), "PR": sb(384, BF), "NEG": sb(8, BF), "BOX": sb(16, BF), "BO2": sb(16, BF), "BOP": sb(8, BF),
    "C2": sb(64, BF), "ZERO": sb(64, BF), "RST": sb(256, F32), "SC": sb(16, F32), "TRI": sb(128, BF),
    "UU1": sb(256, BF), "UU2": sb(128, BF), "MJ1": sb(2, F32), "MJ2": sb(4, F32), "ci": sb(16, I32), "cf": sb(28, F32), "WL": sb(64, F32), "BASE": sb(128, F32),
    "G1": sb(1024, F16), "E": sb(1024, BF), "cb": sb(128, F16), "brep": sb(128, F16), "nbrep": sb(128, F16),
    "CL16": sb(64, U16), "FA16": sb(128, U16), "CH": sb(128, BF), "LX1": sb([16, 2, 8], BF), "LX2": sb([32, 4, 4], BF),
    "P1": sb(256, F32), "t1": sb(256, F32), "s1": sb(128, F32), "s2": sb(128, F32),
    "HT": sb(128, F32), "O16": sb(128, U16), "win": sb(64, F32), "nw": sb(128, F32), "NEW": sb(128, F16),
    "ysend": sb(RO * M, F32),
}
for _s in "01":
    SCRATCH.update({"pl" + _s: sb(8, U16), "c16" + _s: sb(128, U16), "cF" + _s: sb(128, F32), "hr" + _s: sb(128, BF),
                    "sc" + _s: sb(256, F32), "best" + _s: sb(16, I32),
                    "low" + _s: sb(16, I32), "lowb" + _s: sb(16, BF), "sd" + _s: sb(64, F32),
                    "ia" + _s: sb(128, BF), "im" + _s: sb(128, BF), "iF" + _s: sb(128, F32), "ih" + _s: sb(128, BF)})
BANKS = ["SW0", "SW1", "VR00", "VR01", "VR10", "VR11", "K0", "K1"]
for _b in BANKS:
    SCRATCH[_b] = ("psum", [128, 512], F32)
NDMA = 120
SEMAPHORES = ["eV", "eS", "eP", "eG", "sent", "rx", "rst", "ry0", "ry1", "ry2"] + ["d%d" % i for i in range(NDMA)]

FIG = {"cyc": 0.83e-3, "ga": 1.56, "sca": 3.8, "pe": 0.43e-3, "sync": 0.1, "issue": 0.06, "issue_g": 1.0, "land": 2.0, "unit": 235.0}
FIGS = [FIG, dict(FIG, ga=1.2, sca=2.5, pe=0.5e-3), dict(FIG, cyc=1.0e-3, ga=1.95, sca=5.0, pe=0.5e-3, unit=320.0),
        dict(FIG, sync=0.18, issue=0.15, issue_g=1.5, land=3.0, unit=260.0)]
LOOKS, PASSES, MOVES, SLACK, SEED = (0.1, 0.2, 0.3, 0.45), 4, 1500, 0.002, 3
PLAN = {}


def first_new(t):
    return OLD - M * (t + 1)


def lay_out(ops, rank, look, after):
    n = len(ops)
    left, rdy, at = [0] * n, [0.0] * n, [0.0] * n
    for i in range(n):
        for (j, gap) in after[i]:
            left[j] += 1
    ready = dict((e, []) for e in ("V", "S", "P", "G", "Y", "none"))
    free = dict((e, 0.0) for e in ready)
    for i in range(n):
        if not left[i]:
            ready[ops[i]["eng"]].append(i)
    order = []
    while len(order) < n:
        t, e = min((max(free[e], min(rdy[i] for i in l)), e) for e, l in ready.items() if l)
        i = max((j for j in ready[e] if rdy[j] <= t + look), key=lambda j: (rank[j], -j))
        ready[e].remove(i)
        order.append(i)
        at[i] = max(t, rdy[i])
        if e != "none":
            free[e] = at[i] + ops[i]["cost"]
        for (j, gap) in after[i]:
            rdy[j] = max(rdy[j], at[i] + ops[i]["cost"] + gap)
            left[j] -= 1
            if not left[j]:
                ready[ops[j]["eng"]].append(j)
    return max(at[i] + ops[i]["cost"] + ops[i]["lat"] for i in range(n)), order, at


def links(ops, fig):
    succ, pred = [[] for _ in ops], [[] for _ in ops]
    for j, o in enumerate(ops):
        for i in sorted(o["deps"]):
            gap = ops[i]["lat"] + (0.0 if i not in o["hard"] else fig["sync"] / 2 if ops[i]["eng"] == o["eng"] else fig["sync"])
            succ[i].append((j, gap))
            pred[j].append((i, gap))
    return succ, pred


def length(ops, pred, order):
    free, end, last = {}, [0.0] * len(ops), 0.0
    for i in order:
        o = ops[i]
        t = free.get(o["eng"], 0.0)
        for (j, gap) in pred[i]:
            if end[j] + gap > t:
                t = end[j] + gap
        end[i] = t + o["cost"]
        if o["eng"] != "none":
            free[o["eng"]] = end[i]
        last = max(last, end[i] + o["lat"])
    return last


def plan_order(builds):
    ops = builds[0]
    n = len(ops)
    succ, pred = links(ops, FIGS[0])
    preds = [links(b, f)[1] for (b, f) in zip(builds, FIGS)]

    def again(plan, look):
        back = lay_out(ops, [plan[2][i] + ops[i]["cost"] for i in range(n)], look, pred)[2]
        return lay_out(ops, [back[i] + ops[i]["cost"] for i in range(n)], look, succ)

    def score(plan):
        return sum(length(b, p, plan[1]) / f["unit"] for (b, p, f) in zip(builds, preds, FIGS))

    way = [0.0] * n
    for i in range(n - 1, -1, -1):
        way[i] = ops[i]["cost"] + max([way[j] + gap for (j, gap) in succ[i]] + [ops[i]["lat"]])
    plans = []
    for look in LOOKS:
        plans.append(lay_out(ops, way, look, succ))
        for _ in range(PASSES):
            plans.append(again(plans[-1], look))
    cur = min(plans, key=score)
    now = least = score(cur)
    best, parts, seed = cur, sorted(set(o["part"] for o in ops)), [SEED]

    def draw():
        seed[0] = (seed[0] * 1103515245 + 12345) % 2147483648
        return seed[0] / 2147483648

    for _ in range(MOVES):
        lo = draw() * cur[0]
        hi, part, by, look = lo + 5 + 35 * draw(), parts[int(draw() * len(parts))], 12 * (draw() - 0.5), 0.1 + 0.3 * draw()
        at = cur[2]
        plan = lay_out(ops, [0.4 * draw() - at[i] + (by if lo <= at[i] < hi and ops[i]["part"] == part else 0.0) for i in range(n)], look, succ)
        if draw() < 0.3:
            plan = again(plan, look)
        s = score(plan)
        if s <= now + SLACK:
            cur, now = plan, s
        if s < least:
            best, least = plan, s
    return best


def mask_of(engs):
    m = 0
    for e in engs:
        m |= 1 << e
    return m


def widest(engs):
    n = 1
    while 2 * n <= len(engs):
        n *= 2
    return engs[:n]


def build_ops(g, core, T, topo, fig):
    rank = T.rank_of(core)
    CYC, GA, SCA, PEC = fig["cyc"], fig["ga"], fig["sca"], fig["pe"]
    ops, wr_of, rd_of, part = [], {}, {}, ["setup"]
    ALL = 1 << 30

    def tok(x):
        return (x, 0, ALL) if isinstance(x, str) else x

    def add(eng, fn, reads, writes, cost, lat=0.0, kind="c", after=(), sem=None):
        i = len(ops)
        reads = [tok(x) for x in reads]
        writes = [tok(x) for x in writes] + [x for x in reads if x[0] in BANKS]
        reads = [x for x in reads if x[0] not in BANKS]
        deps, hard = set(after), set()
        for (lst, seen) in ((reads, [wr_of]), (writes, [wr_of, rd_of])):
            for (b, lo, hi) in lst:
                for tab in seen:
                    for (j, l2, h2) in tab.get(b, []):
                        if l2 < hi and lo < h2:
                            deps.add(j)
                            if not (b in BANKS and eng == "P" and ops[j]["eng"] == "P"):
                                hard.add(j)
        for (b, lo, hi) in writes:
            wr_of[b] = [w for w in wr_of.get(b, []) if not (lo <= w[1] and w[2] <= hi)] + [(i, lo, hi)]
            rd_of[b] = [w for w in rd_of.get(b, []) if not (lo <= w[1] and w[2] <= hi)]
        for (b, lo, hi) in reads:
            rd_of.setdefault(b, []).append((i, lo, hi))
        ops.append({"eng": eng, "fn": fn, "deps": deps, "hard": hard, "cost": cost, "lat": lat, "kind": kind, "sem": sem,
                    "w": writes[0][0] if writes else "", "part": part[0]})
        return i

    def follow(i, *earlier):
        ops[i]["deps"].update(earlier)

    vq, sq, pq = g.vector, g.scalar, g.tensor

    def vec(fn, r, w, n, per=1.0):
        return add("V", lambda: [fn()], r, w, 0.05 + max(16, n * per) * CYC)

    def act(out, in_, r, w, n, per=1.0, func=ACT.Copy, **kw):
        return add("S", lambda: [sq.activation(out, in_, func, **kw)], r, w, 0.065 + max(16, n * per) * CYC)

    def pool(fn, r, w, n):
        return add("G", lambda: [fn()], r, w, 0.17 + 2 * n * CYC)

    def iota(out, pat, base, w, n):
        return pool(lambda: g.iota(out, pat, base, 0, allow_small_or_imprecise_dtypes=True), [], w, n)

    def mm(lst, r, w, start=True, stop=True):
        cost = sum(max(64, x[3]) * PEC * (4 if x[4] else 1) for x in lst)
        last = len(lst) - 1
        return add("P", lambda: [pq.matmul(x[0], x[1], x[2], start and n == 0, stop and n == last) for n, x in enumerate(lst)],
                   r, w, cost + 0.01)

    def dma(pairs, r, w, us, q="Y", **kw):
        eq = {"Y": g.sync, "S": sq, "G": g}[q]
        return add(q, lambda: [eq.dma_start(o, i, **kw) for (o, i) in pairs], r, w, fig["issue_g" if q == "G" else "issue"] * len(pairs), fig["land"] + us, "dma")

    def copy(out, in_, r, w, n, per=1.0):
        return vec(lambda: vq.tensor_copy(out, in_), r, w, n, per)

    def ts(out, in0, s1, op0, r, w, n, per=1.0, s2=None, op1=None):
        if op1 is None:
            return vec(lambda: vq.tensor_scalar(out, in0, s1, None, op0), r, w, n, per)
        return vec(lambda: vq.tensor_scalar(out, in0, s1, s2, op0, op1), r, w, n, per)

    def tt(out, in0, in1, op, r, w, n, per=2.0):
        return vec(lambda: vq.tensor_tensor(out, in0, in1, op), r, w, n, per)

    def scan(out, d0, d1, r, w, n):
        return vec(lambda: vq.tensor_tensor_scan(out, d0, d1, 0.0, ALU.add, ALU.min), r, w, n)

    def fill(out, val, w, n, per=1.0):
        return vec(lambda: vq.memset(out, val), [], w, n, per)

    def sel(out, in_, pat, cmp, fl, base, cm, r, w, n):
        return pool(lambda: g.affine_select(out, in_, pat, cmp, fl, base, cm), r, w, n)

    def shift(out, in_, bias, r, w, n, **kw):
        return act(out, in_, r, w, n, 1.0, ACT.Identity, bias=bias, **kw)

    def zmat(cls, tgt):
        o = cls * ZW + 15 - tgt
        return T.Z[:, o:o + 128]

    S1, S2 = slice(0, 128, 18), slice(14, 113, 14)
    WO = OLD - PAD
    minus = T.HR[:, 0:128]

    dma([(T.Lraw[:, 64 * k:64 * k + 64], T.nx0[k::8, :]) for k in range(4, 8)], [], [("Lraw", 256, 512)], 0.3)
    dma([(T.Lraw[:, 64 * k:64 * k + 64], T.nx0[k::8, :]) for k in range(4)], [], [("Lraw", 0, 256)], 0.3, "S")
    dma([(T.xc[:, first_new(t):first_new(t) + M], T.x[:, V0 + M * t:V0 + M * t + M]) for t in range(RO)] + [(T.sti[:], T.st[:])],
        [], [("xc", PAD, OLD), "sti"], 0.3)
    dma([(T.xc[:, OLD:U], T.x[:, 0:V0])], [], [("xc", OLD, U)], 0.7)
    dma([(T.NBi[0::2, :], T.nx0[:]), (T.NBi[1::2, :], T.nx0[:])], [], ["NBi"], 1.0)
    fill(T.xc[:, 0:PAD], 0.0, [("xc", 0, PAD)], PAD)
    fill(T.NB0[:, 0:OLD], 0.0, [("NB0", 0, OLD)], OLD)
    fill(T.NB1[:, 0:PAD], 0.0, [("NB1", 0, PAD)], PAD)

    early = [copy(T.st16[:], T.sti[:], ["sti"], ["st16"], 24),
             ts(T.NB0[:, OLD:U], T.NBi[:], float(OLD), ALU.add, ["NBi"], [("NB0", OLD, U), "NB0b"], V0)]

    iota(T.IV[:], [[1, 64], [64, 16]], OLD, ["IV"], V0)
    for h in range(2):
        c = ("Lraw", 256 * h, 256 * h + 256)
        copy(T.L16[:, c[1]:c[2]], T.Lraw[:, c[1]:c[2]], [c], [("L16", c[1], c[2])], 256)

    def slot(k, d):
        return 8 * (k % 2) + 4 * d + k // 2

    def scatter(out, in_, r, w, n, q):
        if q == "S":
            return act(out, in_, r, w, n, SCA, ACT.Silu)
        return copy(out, in_, r, w, n, SCA)

    def invert(k, a, b, q):
        lo = V * slot(k, 1) + WO
        return scatter(T.W[:, lo:lo + V0].indirect(T.L16[:, 64 * k + a:64 * k + b]), T.IV[:, 16 * a:16 * b],
                       ["IV", ("L16", 64 * k, 64 * k + 64)], [("W", lo, lo + V0)], 16 * (b - a), q)

    fill(T.ones[:], 1.0, ["ones"], 1024, 0.5)
    none = act(T.W[:, 0:WO], T.ones[:, 0:WO], ["ones"], [("W", 0, WO)], WO + 1600, 1.0, ACT.Silu, scale=float(NONE))
    invert(4, INV_SPLIT, 64, "V")
    for k in (5, 6, 7):
        follow(invert(k, 0, 64, "V"), *early)
    last = [invert(k, 0, 64, "S") for k in range(4)]
    for i in last:
        follow(i, none)
    follow(invert(4, 0, INV_SPLIT, "S"), *last)
    for k in range(8):
        lo = V * slot(k, 1) + WO
        dma([(T.NB0[2 * k + 1::16, OLD:U], T.W[S2, lo:lo + V0])], [("W", lo, lo + V0)], [("NB0b", OLD + k, OLD + k + 1)], 0.2)

    sent = [0]

    def far(t):
        return T.cores[(rank + 1 + t) % N]

    def near(t):
        return T.cores[(rank - 1 - t) % N]

    def fused(src, offs, dst, width, sem):
        trs = []
        for t in range(RO):
            rid, pid = topo.addr(far(t), core)
            engs = topo.engines(core, far(t))[2 * t:2 * t + 2]
            trs.append(RemoteDMATransfer(dst_ids=[DstId(rid=rid, pnc=pid)], dma_engine_mask=mask_of(engs), remote_sem=sem,
                                         src=src[:, offs[t]:offs[t] + width], dst=dst[:, width * t:width * t + width]))
        sent[0] += 2 * RO
        return lambda: [g.remote_dma_fused(trs, local_sem=T.sem.sent)]

    sx = add("G", fused(T.xc, [first_new(t) for t in range(RO)], T.xr, M, T.sem.rx), [("xc", PAD, OLD)], [], 3.0, 4.0, "remote")
    add("none", None, [], ["xr"], 0.0, 0.0, "recv", [sx], ("rx", 2 * RO))
    ss = add("G", fused(T.st16, [8 * t for t in range(RO)], T.str16, 8, T.sem.rst), ["st16"], [], 1.0, 3.0, "remote")
    follow(ss, sx)
    add("none", None, [], ["str16"], 0.0, 0.0, "recv", [ss], ("rst", 2 * RO))

    ci, cf = T.ci, T.cf

    def col(b, j):
        return b[:, j:j + 1]

    pool(lambda: g.iota(col(ci, 0), [[0, 1]], 0, 1), [], [("ci", 0, 1)], 1)
    vid0 = ("VID", 0, ZW)
    iota(T.VID[:, 0:ZW], [[1, ZW]], 0, [vid0], ZW)
    iota(T.VID[:, ZW:U], [[1, U - ZW]], ZW, [("VID", ZW, U)], U - ZW)
    p = [("ci", 0, 1)]
    ts(col(ci, 1), col(ci, 0), 15, ALU.bitwise_and, p, [("ci", 1, 2)], 1)
    ts(col(ci, 2), col(ci, 0), 1, ALU.bitwise_and, p, [("ci", 2, 3)], 1)
    ts(col(ci, 3), col(ci, 0), 1, ALU.logical_shift_right, p, [("ci", 3, 4)], 1, 1.0, 7, ALU.bitwise_and)
    ts(col(ci, 4), col(ci, 0), 1, ALU.logical_shift_right, p, [("ci", 4, 5)], 1, 1.0, 3, ALU.bitwise_and)
    ts(col(ci, 5), col(ci, 0), 3, ALU.logical_shift_right, p, [("ci", 5, 6)], 1, 1.0, 1, ALU.bitwise_and)
    ts(col(ci, 6), col(ci, 0), 112, ALU.bitwise_and, p, [("ci", 6, 7)], 1)
    ts(col(ci, 8), col(ci, 0), 2, ALU.logical_shift_right, p, [("ci", 8, 9)], 1, 1.0, 3, ALU.bitwise_and)
    ts(col(ci, 9), col(ci, 0), 3, ALU.bitwise_and, p, [("ci", 9, 10)], 1)
    copy(cf[:, 0:7], ci[:, 0:7], ["ci"], [("cf", 0, 7)], 7)
    copy(cf[:, 8:10], ci[:, 8:10], ["ci"], [("cf", 8, 10)], 2)
    c0 = [("cf", 0, 10)]
    ts(col(cf, 7), col(cf, 2), 8.0, ALU.mult, [("cf", 0, 7)], [("cf", 7, 8)], 1, 1.0, col(cf, 3), ALU.add)
    for h in range(HOPS):
        ts(col(cf, 14 + h), col(cf, 7), 64.0, ALU.mult, [("cf", 7, 8)], [("cf", 14 + h, 15 + h)], 1, 1.0, 64.0 * (16 * h + 1) - 128.0, ALU.add)
        ts(col(cf, 17 + h), col(cf, 7), 64.0, ALU.mult, [("cf", 7, 8)], [("cf", 17 + h, 18 + h)], 1, 1.0, 64.0 * (16 * h + 1) + 4112.0, ALU.add)
    ts(col(cf, 11), col(cf, 6), 15.0, ALU.add, c0, [("cf", 11, 12)], 1)
    ts(col(cf, 10), col(cf, 2), 8.0, ALU.mult, c0, [("cf", 10, 11)], 1, 1.0, col(cf, 4), ALU.add)
    for (cj, jj, sl) in ((20, 5, 10), (23, 8, 9)):
        copy(col(cf, cj), col(cf, jj), c0, [("cf", cj, cj + 1)], 1)
        for d in range(2):
            ts(col(cf, cj + 1 + d), col(cf, sl), float(V), ALU.mult, [("cf", 0, 11)], [("cf", cj + 1 + d, cj + 2 + d)], 1, 1.0, 4 * V * d + 0.25 - PAD, ALU.add)
    ts(T.RM[:], T.VID[:, 0:16], col(cf, 1), ALU.is_equal, [vid0, ("cf", 0, 7)], ["RM"], 16)
    for nm in ("Ib", "If", "I16"):
        ts(T[nm][:], T.VID[:, 0:128], col(cf, 0), ALU.is_equal, [vid0, ("cf", 0, 7)], [nm], 128)
    for (o, nm, val) in ((T.Ih[:], "Ih", 0.5), (T.In[:], "In", -0.0625), (T.HR[:, 0:128], ("HR", 0, 128), -1.0),
                         (T.HR[:, 128:256], ("HR", 128, 256), 1.0 / 32), (T.PR[:, 0:128], ("PR", 0, 128), col(cf, 14)),
                         (T.PR[:, 128:256], ("PR", 128, 256), col(cf, 15)), (T.PR[:, 256:384], ("PR", 256, 384), col(cf, 16))):
        ts(o, T.If[:], val, ALU.mult, ["If", "cf"], [nm], 128)
    ts(T.NEG[:], T.VID[:, 0:128:16], col(cf, 0), ALU.is_equal, [vid0, "cf"], ["NEG"], 8, 1.0, -128.0, ALU.mult)
    for c in range(16):
        ts(T.Z[:, c * ZW:c * ZW + ZW], T.VID[:, 0:ZW], col(cf, 11), ALU.is_equal, [vid0, "cf", "RM"], [("Z", c * ZW, c * ZW + ZW)],
           ZW, 1.0, col(T.RM, c), ALU.mult)
    ts(T.Zf[:], T.VID[:, 0:ZW], col(cf, 11), ALU.is_equal, [vid0, "cf", "RM"], ["Zf"], ZW, 1.0, col(T.RM, 0), ALU.mult)
    fill(T.BOX[:], -4096.0, ["BOX"], 16)
    sel(T.BOX[:], T.BOX[:], [[0, 2], [-16, 8]], ALU.is_ge, 0.0, 0, 1, ["BOX"], ["BOX"], 16)
    sel(T.BOX[:], T.BOX[:], [[0, 2], [16, 8]], ALU.is_ge, 0.0, 15, -1, ["BOX"], ["BOX"], 16)
    ts(T.BO2[:], T.BOX[:], -2.0, ALU.mult, ["BOX"], ["BO2"], 16)
    ts(T.BOP[:], T.BOX[:, 0:8], -1.0, ALU.mult, ["BOX"], ["BOP"], 8)
    fill(T.ZERO[:], 0.0, ["ZERO"], 64)
    fill(T.C2[:], -16.0, ["C2"], 64)
    sel(T.C2[:], T.C2[:], [[0, 8], [-16, 8]], ALU.is_ge, 8192.0, 0, 1, ["C2"], ["C2"], 64)
    sel(T.C2[:], T.C2[:], [[0, 8], [16, 8]], ALU.is_ge, 8192.0, 15, -1, ["C2"], ["C2"], 64)
    fill(T.RST[:], 0.0, ["RST"], 256)
    fill(T.RST[:, 0:256:16], BIG, ["RST"], 16)
    fill(T.SC[:, 0:8], 1.0, [("SC", 0, 8)], 8)
    fill(T.SC[:, 8:16], 32.0, [("SC", 8, 16)], 8)
    sel(T.SELU[:], T.ones[:], [[-16, 8], [0, 8], [-1, 16]], ALU.is_equal, 0.0, 0, 1, ["ones"], ["SELU"], 1024)
    sel(T.E[:], T.ones[:], [[-16, 8], [0, 128]], ALU.is_equal, 0.0, 0, 1, ["ones"], ["E"], 1024)
    copy(T.SEL[:], T.E[:], ["E"], ["SEL"], 1024, 0.5)
    fill(T.TRI[:], 4096.0, ["TRI"], 128, 0.5)
    sel(T.TRI[:], T.TRI[:], [[-1, 128]], ALU.is_ge, 0.0, 0, 1, ["TRI"], ["TRI"], 128)
    for hv in sorted(set(HALVES)):
        uu, jj, uw = "UU%d" % hv, 2 * hv, 64 // hv
        sel(T[uu][:, 0:2 * uw], T.ones[:, 0:2 * uw], [[0, 2], [-jj, uw]], ALU.is_ge, 0.0, 0, 1, ["ones"], [(uu, 0, 2 * uw)], 2 * uw)
        sel(T[uu][:, 0:2 * uw], T[uu][:, 0:2 * uw], [[0, 2], [jj, uw]], ALU.is_ge, 0.0, jj - 1, -1, [(uu, 0, 2 * uw)], [(uu, 0, 2 * uw)], 2 * uw)
        for d in range(2):
            ts(T[uu][:, (2 + d) * uw:(3 + d) * uw], T[uu][:, 0:uw], 4.0 * V * (1 - 2 * d), ALU.mult, [(uu, 0, 2 * uw)], [(uu, (2 + d) * uw, (3 + d) * uw)], uw, 0.5)
        ts(T["MJ%d" % hv][:], T.VID[:, 0:jj], col(cf, (2, 9)[hv - 1]), ALU.is_equal, [vid0, "cf"], ["MJ%d" % hv], jj)

    iota(T.W[:, WO:V], [[0, V0]], NONE, [("W", WO, V)], V0)
    nxs, pvs = [slot(k, 0) for k in range(1, 8)], [slot(k, 1) for k in range(8)]
    dma([(T.W[:, V * c:V * c + V], T.W[:, 0:V]) for c in nxs] + [(T.W[:, V * c:V * c + WO], T.W[:, 0:WO]) for c in pvs], [("W", 0, V), "NB0b"],
        [("W", V * c, V * c + V) for c in nxs] + [("W", V * c, V * c + WO) for c in pvs], 11.0)
    dma([(T.W[S1, V * slot(k, 0) + WO:V * slot(k, 0) + V], T.NB0[2 * k::16, OLD:U]) for k in range(8)], ["NB0"],
        [("W", V * slot(k, 0), V * slot(k, 0) + V) for k in range(8)], 1.5)
    dma([(T.yA[:, OLD:U], T.y0[:])], [], [("yA", OLD, U)], 1.5, "G")

    def nb_of(t):
        nm = "NB%d" % (t % 2)
        return T[nm], [nm, nm + "b"]

    def search_steps(t, s):
        new = first_new(t)
        xv, xn = (T.xc[:, new:new + M], "xc") if s == 0 else (T.xr[:, M * t:M * t + M], "xr")
        st, sn = (T.st16, "st16") if s == 0 else (T.str16, "str16")
        st = st[:, 8 * t:8 * t + 8]
        n = dict((k, k + str(s)) for k in ("pl", "c16", "cF", "hr", "sc", "best", "low", "lowb", "sd", "ia", "im", "iF", "ih", "d", "r", "ve", "K"))
        b = dict((k, T[v]) for k, v in n.items())
        xw, K = T.xc[:], b["K"]
        nb, nbn = nb_of(t)
        nv, nm = ON_VECTOR[t][s], MIXED[t][s]

        def begin():
            ve = b["ve"]
            for c in (0, 8):
                sel(ve[:, c:2048:16], xv, [[0, M]], ALU.is_equal, 0.0, 0, 0, [xn], [n["ve"]], M)
            for c in (8, 4, 2):
                sel(ve[:, c // 2:2048:c], ve[:, 0:2048:c], [[0, 2048 // c]], ALU.is_equal, 0.0, 0, 0, [n["ve"]], [n["ve"]], 2048 // c)
            tt(b["ia"][:], T.xc[:, OLD:U].indirect(st), ve[:, 0:2048:16], ALU.subtract, ["xc", n["ve"], sn], [n["ia"]], 128, GA)
            ts(b["im"][:], b["ia"][:], 0.0, ALU.max, [n["ia"]], [n["im"]], 128, 0.5)
            act(b["iF"][:], T.VID[:, OLD:U].indirect(st), ["VID", sn], [n["iF"]], 128, GA, ACT.Identity, bias=4112.0)
            act(b["ih"][:], T.VID[:, OLD:U].indirect(st), ["VID", sn], [n["ih"]], 128, GA, ACT.Identity, bias=4096.0)
            mm([(K[:, 0:16], b["ih"][:], T.HR[:, 0:256:16], 16, False), (K[:, 0:8], b["iF"][:], T.If[:, 0:128:16], 8, True),
                (K[:, 8:16], T.ones[:, 0:128], T.NEG[:], 8, False),
                (K[:, 0:16], b["ia"][:], T.BOX[:], 16, False), (K[:, 0:16], b["im"][:], T.BO2[:], 16, False)],
               [n["ih"], n["iF"], n["ia"], n["im"], "HR", "If", "ones", "NEG", "BOX", "BO2"], [n["K"]])
            copy(b["best"][:], K[:, 0:16], [n["K"]], [n["best"]], 16)

        def step(h):
            at, rd = (nb[:, OLD:U].indirect(st), [(x, OLD, U) for x in nbn] + [sn]) if h == 0 else (nb[:].indirect(b["pl"][:]), nbn + [n["pl"]])
            ts(b["c16"][:], at, 0.25, ALU.add, rd, [n["c16"]], 128, GA)
            act(b["hr"][:], at, rd, [n["hr"]], 128, GA, ACT.Identity, bias=4096.0)
            act(b["cF"][:], at, rd + ["cf"], [n["cF"]], 128, GA, ACT.Identity, bias=col(cf, 17 + h))
            mm([(K[:, 0:256], b["hr"][:], T.HR[:], 256, False), (K[:, 0:128], b["cF"][:], T.If[:], 128, True),
                (K[:, 128:256], T.ones[:, 0:128], T.PR[:, 128 * h:128 * h + 128], 128, False)],
               [n["hr"], n["cF"], "HR", "If", "ones", "PR"], [n["K"]], True, False)
            for (lo, hi, mixed) in ((512 * nv, 512 * (nv + nm), True), (0, 512 * nv, False)):
                if lo == hi:
                    continue
                td, tr = (n["d"], lo, hi), (n["r"], lo, hi)
                tt(b["d"][:, lo:hi], xw.indirect(b["c16"][:, lo // 16:hi // 16]), b["ve"][:, lo:hi], ALU.subtract, ["xc", n["c16"], n["ve"]], [td], hi - lo, GA)
                if mixed:
                    act(b["r"][:, lo:hi], b["d"][:, lo:hi], [td], [tr], hi - lo, 1.0, ACT.Abs, scale=0.5)
                else:
                    ts(b["r"][:, lo:hi], b["d"][:, lo:hi], 0.0, ALU.max, [td], [tr], hi - lo, 0.5)
                    mm([(K[0:32 * nv, c:256:16], b["d"][:, c:hi:16], T.BOX[:], 16, False) for c in range(16)], [td, "BOX"], [n["K"]], False, False)
            for q in range(nv + nm, 4):
                lo, vr = 512 * q, "VR%d%d" % (s, q % 2)
                td, tr = (n["d"], lo, lo + 512), (n["r"], lo, lo + 512)
                act(b["d"][:, lo:lo + 512], xw.indirect(b["c16"][:, 32 * q:32 * q + 32]), ["xc", n["c16"]], [td], 512, GA)
                mm([(T[vr][:], T.Ib[:], b["d"][:, lo:lo + 512], 512, False), (T[vr][:], minus, b["ve"][:, lo:lo + 512], 512, False)],
                   [td, n["ve"], "Ib", "HR"], [vr])
                act(b["r"][:, lo:lo + 512], T[vr][:], [vr], [tr], 512, 1.0, ACT.Abs, scale=0.5)
            mm([(K[:, c:256:16], b["r"][:, c:2048:16], T.BO2[:], 16, False) for c in range(16)], [n["r"], "BO2"], [n["K"]], False, True)
            scan(b["sc"][:], T.RST[:], K[:, 0:256], ["RST", n["K"]], [n["sc"]], 256)
            tt(b["best"][:], b["sc"][:, 15:256:16], b["best"][:], ALU.min, [n["sc"], n["best"]], [n["best"]], 16)
            ts(b["low"][:], b["best"][:], 63, ALU.bitwise_and, [n["best"]], [n["low"]], 16)
            tt(b["lowb"][:], b["low"][:], T.SC[:], ALU.mult, [n["low"], "SC"], [n["lowb"]], 16)
            mm([(K[:, 0:64], T.Ib[:], T.C2[:], 64, False)] +
               [(K[:, 8 * u:8 * u + 8], T.SELU[:, 128 * u:128 * u + 128], b["lowb"][:, 8 * w:8 * w + 8], 8, False) for u in range(8) for w in range(2)],
               ["Ib", "C2", "SELU", n["lowb"]], [n["K"]])
            scan(b["sd"][:], T.RST[:, 0:128:2], K[:, 0:64], ["RST", n["K"]], [n["sd"]], 64)
            ts(b["pl"][:], b["sd"][:, 7:64:8], -float(new + M) if s == 1 and h == HOPS - 1 else 0.0, ALU.add, [n["sd"]], [n["pl"]], 8)

        return begin, step

    def send_y(t):
        new = first_new(t)
        src = T.ysend[:, M * t:M * t + M]
        if EARLY[t]:
            nb, nbn = nb_of(t)
            yw, ty = T.yB[:, new + M:U], ("yB", new + M, U)
            ts(T.c161[:], nb[:, new + M:U].indirect(T.pl1[:]), 0.25 - new - M, ALU.add, nbn + ["pl1"], ["c161"], 128, GA)
            act(T.cF1[:], yw.indirect(T.pl1[:]), [ty, "pl1"], ["cF1"], 128, GA)
            mm([(T.K1[:, 0:128], T.Ih[:], T.cF1[:], 128, True)], ["Ih", "cF1"], ["K1"], True, False)
            for x in range(2):
                at, tp = ring(1024)
                act(T.PS[:, at:at + 1024], yw.indirect(T.c161[:, 64 * x:64 * x + 64]), [ty, "c161"], [tp], 1024, GA)
                tt(T.PS[:, at:at + 1024:2], T.PS[:, at:at + 1024:2], T.PS[:, at + 1:at + 1024:2], ALU.mult, [tp], [tp], 512)
                mm([(T.K1[:, 64 * x:64 * x + 64], T.In[:], T.PS[:, at + 2 * k:at + 1024:16], 64, True) for k in range(8)], [tp, "In"], ["K1"], False, x == 1)
            shift(src, T.K1[:, 0:128], 0.5, ["K1"], [("ysend", M * t, M * t + M)], 128)
        else:
            act(src, T.yA[:, new + M:U].indirect(T.pl1[:]), [("yA", new + M, U), "pl1"], [("ysend", M * t, M * t + M)], 128, GA)
        rid, pid = topo.addr(near(t), core)
        engs = widest(topo.engines(core, near(t)))
        sem = T.sem["ry%d" % t]
        sent[0] += len(engs)
        s = add("G", lambda: [g.remote_dma(T.yA[:, new:new + M], src, sem, T.sem.sent, pid, rid, mask_of(engs))],
                [("ysend", M * t, M * t + M)], [], 1.0, 3.5, "remote")
        add("none", None, [], [("yA", new, new + M)], 0.0, 0.0, "recv", [s], ("ry%d" % t, len(widest(topo.engines(far(t), core)))))

    def enter(t):
        new = first_new(t)
        now = U - new
        nb, nbn = nb_of(t)
        pl, xw = T.pl0[:], T.xc[:]
        nn = "NB%d" % ((t + 1) % 2)
        HV = HALVES[t]
        KK, JJ = 8 // HV, 2 * HV
        UW, GW, n = M // JJ, 8 * KK, 1024 // HV
        jk = [(jj, kk) for jj in range(JJ) for kk in range(KK)]
        cj, LX, lx, UU, uu, MJ, mj = 20 + 3 * (HV - 1), T["LX%d" % HV], "LX%d" % HV, T["UU%d" % HV], "UU%d" % HV, T["MJ%d" % HV], "MJ%d" % HV
        iota(T.WENC[:, 0:n], [[1, 128], [0, KK]], new, ["WENC"], n)
        for e in range(HV):
            shift(T.WL[:, UW * e:UW * e + UW], T.VID[:, new:new + M:JJ], col(cf, cj), ["VID", "cf"], [("WL", UW * e, UW * e + UW)], UW)
        wl, twl = T.WL[:, 0:UW], ("WL", 0, UW)
        for d in range(2):
            shift(T.BASE[:, UW * d:UW * d + UW], wl, col(cf, cj + 1 + d), [twl, "cf"], [("BASE", UW * d, UW * d + UW)], UW)
        copy(T.cb[:], nb[:].indirect(pl), nbn + ["pl0"], ["cb"], 128, GA)
        copy(T.brep[:], T.VID[:].indirect(pl), ["VID", "pl0"], ["brep"], 128, GA)
        ts(T.nbrep[:], T.brep[:], -1.0, ALU.mult, ["brep"], ["nbrep"], 128, 0.5)
        for x in range(2):
            vr = "VR0%d" % x
            lst = [(T[vr][:], T.nbrep[:], T.SEL[:, 512 * x:512 * x + 512], 512, False)]
            for q in range(4):
                o = T[vr][:, 128 * q:128 * q + 128]
                lst += [(o, T.SEL[:, 512 * x + 128 * q:512 * x + 128 * q + 128], T.brep[:], 128, False), (o, T.Ib[:], T.TRI[:], 128, False)]
            mm(lst, ["nbrep", "brep", "SEL", "Ib", "TRI"], [vr])
            ts(T.E[:, 512 * x:512 * x + 512], T[vr][:], 0.0, ALU.is_equal, [vr], [("E", 512 * x, 512 * x + 512)], 512)
        neg = T.BOX[:, 0:8]

        def half(e):
            kn, rn = (("K0", "VR00"), ("SW0", "SW1"))[e]
            K, R = T[kn], T[rn]

            def piece(nm, per, a, z):
                lo, hi = UW * (per * e + a), UW * (per * e + z)
                return T[nm][:, lo:hi], (nm, lo, hi)

            mm([(R[:, 0:UW], zmat(2 * ((HV * kk + e + 1) % 8), KK * jj + kk), T.cb[:, jj:128:JJ], UW, False) for (jj, kk) in jk], ["Z", "cb"], [rn])
            (cl, tcl), (fa, tfa), pp = piece("CL16", 1, 0, 1), piece("FA16", 2, 0, 2), [piece("P1", 4, x, x + 1) for x in range(4)]
            copy(cl, R[:, 0:UW], [rn], [tcl], UW)
            tt(pp[0][0], R[:, 0:UW], wl, ALU.subtract, [rn, twl], [pp[0][1]], UW, 1.0)
            act(pp[2][0], pp[0][0], [pp[0][1]], [pp[2][1]], UW)
            tg = ("G1", n * e, n * e + n)
            copy(T.G1[:, n * e:n * e + n], nb[:].indirect(cl), nbn + [tcl], [tg], n, GA)
            for d in range(2):
                mm([(K[:, UW * d:UW * d + UW], zmat(2 * (HV * kk + e) + d, KK * jj + kk), T.G1[:, n * e + KK * jj + kk:n * e + n:16], UW, False)
                    for (jj, kk) in jk], ["Z", tg], [kn])
            copy(fa, K[:, 0:2 * UW], [kn], [tfa], 2 * UW)
            for d in range(2):
                tt(pp[1 + 2 * d][0], K[:, UW * d:UW * d + UW], wl, ALU.subtract, [kn, twl], [pp[1 + 2 * d][1]], UW, 1.0)
            mm([(K[:, 0:GW], T.Ib[:], T.ZERO[:, 0:GW], GW, False)], ["Ib", "ZERO"], [kn], True, False)
            for d in range(2):
                lo = n * (2 * e + d)
                act(T.d0[:, lo:lo + n], xw.indirect(piece("FA16", 2, d, d + 1)[0]), ["xc", tfa], [("d0", lo, lo + n)], n, GA)
                tt(T.r0[:, lo:lo + n], xw.indirect(cl), T.d0[:, lo:lo + n], ALU.max, ["xc", tcl, ("d0", lo, lo + n)], [("r0", lo, lo + n)], n, GA)
                for q in range(n // 512):
                    a, vr = lo + 512 * q, ("VR01", rn)[(d + q) % 2]
                    mm([(T[vr][:], T.Ib[:], T.d0[:, a:a + 512], 512, False), (T[vr][:], minus, T.ve0[:, 512 * JJ * q:512 * JJ * (q + 1):JJ], 512, False)],
                       [("d0", a, a + 512), "ve0", "Ib", "HR"], [vr])
                    act(T.mv[:, a:a + 512], T[vr][:], [vr], [("mv", a, a + 512)], 512, 1.0, ACT.Relu)
                for (nm, sign) in (("r0", (T.BOP[:], neg)[d]), ("mv", (neg, T.BOP[:])[d])):
                    mm([(K[:, kk:GW:KK], T[nm][:, lo + kk:lo + n:KK], sign, 8, False) for kk in range(KK)], [(nm, lo, lo + n), "BOX", "BOP"], [kn],
                       False, nm == "mv" and d == 1)
            ch, tch = 2 * GW * e, ("CH", 2 * GW * e, 2 * GW * e + 2 * GW)
            ts(T.CH[:, ch:ch + GW], K[:, 0:GW], 0.0, ALU.is_ge, [kn], [("CH", ch, ch + GW)], GW)
            ts(T.CH[:, ch + GW:ch + 2 * GW], K[:, 0:GW], 0.0, ALU.is_lt, [kn], [("CH", ch + GW, ch + 2 * GW)], GW)
            mm([(K[:, 4 * UW:6 * UW], T.If[:], T.BASE[:, 0:2 * UW], 2 * UW, True)], ["If", "BASE"], [kn], True, False)
            for w in range(2):
                own, other = ch + GW * w, ch + GW * (1 - w)
                mm([(R[:, GW * w:GW * w + GW], T.Ib[:], T.CH[:, other:other + GW], GW, False)] +
                   [(R[:, GW * w + KK * q:GW * w + KK * q + KK], T.E[:, 128 * q:128 * q + 128], T.CH[:, own + KK * q:own + KK * q + KK], KK, False)
                    for q in range(8)], ["Ib", tch, "E"], [rn])
            for jj in range(JJ):
                ts(LX[:, 16 * e:16 * e + 16, jj, :], R[:, 0:2 * GW], 0.0, ALU.is_equal, [rn, mj], [(lx, JJ * e + jj, JJ * e + jj + 1)], 2 * GW,
                   1.0, col(MJ, jj), ALU.mult)
            ahead, back, tlx = LX[:, 16 * e:16 * e + 8, :, :], LX[:, 16 * e + 8:16 * e + 16, :, :], (lx, JJ * e, JJ * e + JJ)
            mm([(K[:, 4 * UW:6 * UW], back, UU[:, 2 * UW:4 * UW], 2 * UW, False)], [tlx, uu], [kn], False, True)
            mm([(K[:, 0:2 * UW], ahead, UU[:, 0:2 * UW], 2 * UW, False)], [tlx, uu], [kn])
            mm([(K[:, 2 * UW:4 * UW], back, UU[:, 0:2 * UW], 2 * UW, False)], [tlx, uu], [kn])
            (t1, tt1), (s1, ts1), (s2, ts2), (o16, to) = piece("t1", 4, 0, 4), piece("s1", 2, 0, 2), piece("s2", 2, 0, 2), piece("O16", 2, 0, 2)
            tt(t1, K[:, 0:4 * UW], piece("P1", 4, 0, 4)[0], ALU.mult, [kn, piece("P1", 4, 0, 4)[1]], [tt1], 4 * UW, 1.0)
            tt(s1, piece("t1", 4, 0, 2)[0], piece("t1", 4, 2, 4)[0], ALU.add, [tt1], [ts1], 2 * UW)
            tt(s2, s1, K[:, 4 * UW:6 * UW], ALU.add, [ts1, kn], [ts2], 2 * UW, 1.0)
            copy(o16, s2, [ts2], [to], 2 * UW)
            for d, (x, y) in enumerate(((1, 2), (0, 3))):
                lo = 64 * d + UW * e
                tt(T.HT[:, lo:lo + UW], piece("t1", 4, x, x + 1)[0], piece("t1", 4, y, y + 1)[0], ALU.add, [tt1], [("HT", lo, lo + UW)], UW)
            wa, wz = 16 * V // HV * e, 16 * V // HV * (e + 1)
            win, tw, iv, ti = T.W[:, wa:wz], ("W", wa, wz), T.IV[:, n * e:n * e + n], ("IV", n * e, n * e + n)
            near_end, far_end = piece("O16", 2, 0, 1)[0], piece("O16", 2, 1, 2)[0]
            scatter(win.indirect(near_end), T.WENC[:, 0:n], [to, "WENC"], [tw], n, SCATTERS[t][2 * e])
            tt(iv, win.indirect(far_end), T.WENC[:, 0:n], ALU.min, [tw, to, "WENC"], [ti], n, GA)
            scatter(win.indirect(far_end), iv, [to, ti], [tw], n, SCATTERS[t][2 * e + 1])
            mine = range(2) if HV == 1 else [e]
            dma([(T[nn][2 * x + d::4, PAD:U], T.W[(S1, S2)[d], V * (8 * x + 4 * d):V * (8 * x + 4 * d + 4)]) for x in mine for d in range(2)],
                [tw], [(nn + ("", "b")[x], PAD, U) for x in mine], 1.3 / HV)

        for e in range(HV):
            half(e)
        K, R = T.K0, T.VR00
        mm([(R[:, 0:64], T.Zf[:, 15 - c:143 - c], T.IV[:, c:1024:16], 64, True) for c in range(16)], ["Zf", "IV"], ["VR00"])
        tt(T.win[:], R[:, 0:64], T.WL[:], ALU.is_equal, ["VR00", "WL"], ["win"], 64, 1.0)
        for d in range(2):
            lo = 64 * d
            tt(T.nw[:, lo:lo + 64], T.win[:], T.HT[:, lo:lo + 64], ALU.mult, ["win", "HT"], [("nw", lo, lo + 64)], 64)
            tt(T.NEW[:, lo:lo + 64], T.nw[:, lo:lo + 64], T.WL[:], ALU.add, [("nw", lo, lo + 64), "WL"], [("NEW", lo, lo + 64)], 64)
        for jj in range(JJ):
            mm([(K[:, jj:128:JJ], zmat(KK * jj + kk, 2 * (HV * kk + e) + d), T.NEW[:, 64 * d + UW * e:64 * d + UW * e + UW], UW, False)
                for kk in range(KK) for e in range(HV) for d in range(2)], ["Z", "NEW"], ["K0"])
        act(T[nn][:, new:new + M], K[:, 0:128], ["K0"], [(nn, new, new + M), (nn + "b", new, new + M)], 128)
        if t:
            both = [(nn, new + M, OLD), (nn + "b", new + M, OLD)]
            tt(T[nn][:, new + M:OLD], T[nn][:, new + M:OLD], nb[:, new + M:OLD], ALU.min, both + nbn, both, M * t)
        Q, ls = now // 4, "LS%d" % (t % 2)
        for q in range(4):
            ts(T.NB16[:, Q * q:Q * q + Q], T[nn][:, new + q:U:4], 0.25 - new, ALU.add, [nn, nn + "b"], [("NB16", Q * q, Q * q + Q)], Q)
        for d in range(2):
            dma([(T[ls][kk::4, QM * (2 * d + e):QM * (2 * d + e) + Q], T.NB16[4 * kk + 2 * e + d::16, 0:now]) for e in range(2) for kk in range(4)],
                ["NB16"], [(ls, 2 * QM * d, 2 * QM * d + 2 * QM)], 0.3)
        if t + 1 == RO:
            put_nx(T[nn], nn)

    def put_nx(nb, nn):
        H = V // 2
        dma([(T.IV[0::2, 0:H], nb[0::2, OLD:OLD + H]), (T.IV[1::2, 0:V0 - H], nb[0::2, OLD + H:U])] +
            [(T.IV[1::2, V0 - H + M * t:V0 - H + M * t + M], nb[0::2, first_new(t):first_new(t) + M]) for t in range(RO)], [nn, nn + "b"], ["IV"], 0.5)
        num = T.Z[:, 0:H]
        copy(num, T.IV[:, 0:H], ["IV"], ["Z"], H)
        parts = [(T.d0[:, 0:H], ("d0", 0, H), first_new(1), 2 * M), (T.d0[:, H:V], ("d0", H, V), first_new(0), 2 * M), (T.r0[:, 0:H], "r0", OLD, V0 + M)]
        for (o, nm, edge, drop) in parts:
            ts(o, num, float(edge), ALU.is_ge, ["Z"], [nm], H, 0.5, -float(drop), ALU.mult)
        for x in range(2):
            lo, vr = QM * x, "VR0%d" % x
            o = T[vr][:, 0:QM]
            mm([(o, T.I16[:], T.Z[:, lo:lo + QM], QM, False), (o, T.Ib[:], T.d0[:, lo:lo + QM], QM, False),
                (o, T.Ib[:], T.d0[:, H + lo:H + lo + QM], QM, False), (o, T.Ib[:], T.r0[:, lo:lo + QM], QM, False)], ["I16", "Ib", "Z", "d0", "r0"], [vr])
            shift(T.WENC[:, lo:lo + QM], o, float(V - M - PAD), [vr], [("WENC", lo, lo + QM)], QM)
        dma([(T.nx[:], T.WENC[:, 0:H])], ["WENC"], [], 0.7)

    def put_y(lo, hi):
        pairs = []
        while lo < hi:
            if lo >= OLD:
                end, to = hi, lo - OLD
            else:
                blk = (lo - PAD) // M
                end, to = min(hi, PAD + M * blk + M), V0 + M * (RO - 1 - blk) + lo - PAD - M * blk
            pairs.append((T.y[:, to:to + end - lo], T.yA[:, lo:end]))
            lo = end
        return pairs

    turn = [0, 0]

    def ring(n):
        if turn[1] + n > RING:
            turn[1] = 0
        turn[1] += n
        return turn[1] - n, ("PS", turn[1] - n, turn[1])

    def sweeps(t):
        new = first_new(t)
        ls = "LS%d" % (t % 2)
        banks = SWEEP_BANKS[t]
        if SCANS[t]:
            sel(T.E[:], T.ones[:], [[0, 256], [1, 4]], ALU.is_gt, 0.0, 0, 0, ["ones"], ["E"], 1024)
        for s in range(SWEEPS):
            src, dst = ("yA", "yB") if s == 0 else ("yB", "yA")
            yw, ty = T[src][:, new:U], (src, new, U)
            u = 0
            for c, wd in enumerate(CHUNKS[t]):
                if s == SWEEPS - 1 and t + 1 < RO and EARLY[t + 1] == c + 1:
                    send_y(t + 1)
                n = 16 * wd
                bank = banks[turn[0] % len(banks)]
                turn[0] += 1
                lo, hi = new + 4 * u, new + 4 * (u + wd)
                o = T[bank][:, 0:4 * wd]
                mm([(o, T.Ih[:], T[src][:, lo:hi], 4 * wd, True)], [(src, lo, hi), "Ih"], [bank], True, False)
                for e in range(2):
                    at, tp = ring(n)
                    P = T.PS[:, at:at + n]
                    la, lb = QM * e + u, QM * (2 + e) + u
                    act(P, yw.indirect(T[ls][:, la:la + wd]), [ty, (ls, la, la + wd)], [tp], n, GA)
                    tt(P, yw.indirect(T[ls][:, lb:lb + wd]), P, ALU.mult, [ty, (ls, lb, lb + wd), tp], [tp], n, GA)
                    picks = range(4)
                    if c in BY_DMA[t]:
                        if e == 0:
                            even = (at, tp, P)
                            continue
                        dma([(even[2], P)], [even[1], tp], [even[1]], n * 1.7e-3, "G", accum_op=ALU.add)
                        at, tp = even[0], even[1]
                    if (c, e) in SCANS[t]:
                        at, tq = ring(n)
                        vec(lambda o=T.PS[:, at:at + n], P=P, n=n: vq.tensor_tensor_scan(o, T.E[:, 0:n], P, 0.0, ALU.mult, ALU.add), [tp, "E"], [tq], n)
                        tp, picks = tq, [3]
                    mm([(o, T.In[:], T.PS[:, at + kk:at + n:4], 4 * wd, True) for kk in picks], [tp, "In"], [bank], False, e == 1)
                if EVAC[t][c % len(EVAC[t])] == "V":
                    ts(T[dst][:, lo:hi], o, 0.5, ALU.add, [bank], [(dst, lo, hi)], 4 * wd)
                else:
                    shift(T[dst][:, lo:hi], o, 0.5, [bank], [(dst, lo, hi)], 4 * wd)
                if t == RO - 1 and s == SWEEPS - 1:
                    dma(put_y(lo, hi), [(dst, lo, hi)], [], 0.3)
                u += wd

    def searches(t):
        for s in range(2):
            part[0] = ("own", "served")[s] + str(t)
            begin, step = search_steps(t, s)
            begin()
            for h in range(HOPS):
                step(h)

    searches(0)
    send_y(0)
    for t in range(RO):
        part[0] = "enter" + str(t)
        enter(t)
        if t + 1 < RO:
            searches(t + 1)
        part[0] = "sweeps" + str(t)
        sweeps(t)
        if t + 1 < RO and not EARLY[t + 1]:
            send_y(t + 1)
    return ops, sent[0]


def rank_program(g, core, T, topo):
    if T.rank_of(core) is None:
        return
    ops, sent = build_ops(g, core, T, topo, FIG)
    if "order" not in PLAN:
        PLAN["order"] = plan_order([build_ops(g, core, T, topo, f)[0] for f in FIGS])[1]
    queue = {"V": g.vector, "S": g.scalar, "P": g.tensor, "G": g, "Y": g.sync}
    count = {"V": 0, "S": 0, "P": 0, "G": 0}
    waited = dict((q, {}) for q in queue)
    final, ndma = {}, [0]
    for i in PLAN["order"]:
        o = ops[i]
        if o["kind"] == "recv":
            o["done"] = o["sem"]
            final[o["sem"][0]] = o["sem"][1]
            continue
        q = queue[o["eng"]]
        need = {}
        for d in o["hard"]:
            name, val = ops[d]["done"]
            need[name] = max(need.get(name, 0), val)
        for name in sorted(need):
            if waited[o["eng"]].get(name, 0) < need[name]:
                q.wait_ge(T.sem[name], need[name])
                waited[o["eng"]][name] = need[name]
        ins = o["fn"]()
        if o["kind"] == "dma":
            name = "d%d" % ndma[0]
            ndma[0] += 1
            for x in ins:
                x.then_inc(T.sem[name], 16)
            o["done"] = (name, 16 * len(ins))
        elif o["kind"] == "remote":
            o["done"] = ("sent", sent)
        else:
            name = "e" + o["eng"]
            for x in ins:
                x.then_inc(T.sem[name], 1)
            count[o["eng"]] += len(ins)
            o["done"] = (name, count[o["eng"]])
        final[o["done"][0]] = max(final.get(o["done"][0], 0), o["done"][1])
    for name in sorted(final):
        if waited["G"].get(name, 0) < final[name]:
            g.wait_ge(T.sem[name], final[name])
